import numpy as np
import ml_dtypes


def mxq(x, axis, fmt="e4m3"):
    dtype, down = {"e4m3": (ml_dtypes.float8_e4m3fn, 7), "e5m2": (ml_dtypes.float8_e5m2, 14)}[fmt]
    v = np.moveaxis(np.asarray(x, np.float32).astype(ml_dtypes.bfloat16).astype(np.float64), axis, -1)
    blocks = v.reshape(v.shape[:-1] + (-1, 32))
    amax = np.abs(blocks).max(-1, keepdims=True)
    byte = np.maximum(np.where(amax > 0, np.frexp(amax)[1] - 1 + 127, 0) - down, 1)
    scale = np.exp2(byte - 127.0)
    codes = (blocks / scale).astype(np.float32).astype(dtype).astype(np.float64)
    return np.moveaxis((codes * scale).reshape(v.shape), -1, axis)


WIDE = False


def mx_kscale(k):
    if not WIDE:
        return np.ones(k)
    levels = np.array([10, -10, 5, -5, 0])
    if k % 512:
        return np.exp2(np.random.permutation(np.resize(levels, k // 32))).repeat(32)
    a = np.empty((k // 512, 16))
    for p in range(k // 512):
        a[p, :8] = np.random.permutation(np.resize(levels, 8))
        for g in range(8):
            far = levels[np.abs(levels - a[p, g]) >= 10]
            a[p, g + 8] = far[np.random.randint(len(far))]
    return np.exp2(a.ravel()).repeat(32)


def f64(x):
    return np.asarray(x).astype(np.float64)


def striped(idx):
    return np.tile(idx.reshape(-1, 16).T, (8, 1)).astype(np.uint16)


def unstriped(offs):
    return offs[:16].T.reshape(-1).astype(np.int64)


def pack_weight(w):
    k, n = w.shape
    w = f64(np.asarray(w, np.float32).astype(ml_dtypes.bfloat16)).reshape(k // 32, 32, n)
    amax = np.abs(w).max(1)
    byte = np.clip(np.where(amax > 0, np.frexp(amax)[1] - 1 + 127 - 7, 1), 1, 254)
    scaled = (w * np.exp2(127.0 - byte)[:, None, :]).reshape(k, n).astype(np.float32)
    words = np.ascontiguousarray(scaled.reshape(k // 512, 128, 4, n).transpose(0, 1, 3, 2)).astype(ml_dtypes.float8_e4m3fn).view(np.uint8)
    return words, np.ascontiguousarray(byte.astype(np.uint8).reshape(k // 512, 16, n))


def unpack_weight(words, scales):
    g, p, n, _ = words.shape
    vals = np.ascontiguousarray(words).view(ml_dtypes.float8_e4m3fn).astype(np.float64) * np.repeat(np.exp2(scales.astype(np.float64) - 127.0), 8, axis=1)[..., None]
    return vals.transpose(0, 1, 3, 2).reshape(g * 512, n)


def planes(y):
    n, m = y.shape
    v = y.astype(np.float32).astype(ml_dtypes.bfloat16).astype(np.float64).reshape(n // 32, 32, m)
    top = np.abs(v).max(1)
    byte = np.clip(np.where(top > 0, np.frexp(top)[1] - 1 + 127 - 7, 1), 1, 254)
    codes = (v * np.exp2(127.0 - byte)[:, None, :]).reshape(n, m).astype(np.float32).astype(ml_dtypes.float8_e4m3fn).view(np.uint8)
    words = codes.reshape(n // 512, 128, 4, m).transpose(0, 1, 3, 2)
    return np.ascontiguousarray(words), np.ascontiguousarray(byte.astype(np.uint8).reshape(n // 512, 16, m))


def relu(v):
    return np.maximum(v, 0.0)


K, T, S, V, D, N = 1024, 4096, 1024, 256, 3, 512
P = 2 ** 7


def setup_inputs():
    n = np.random.standard_normal
    s = mx_kscale(K)[:, None]
    packed_xT = pack_weight(n((K, T)) * s)
    return {
        "x_words": packed_xT[0],
        "x_scales": packed_xT[1],
        "w0": (n((K, N)) / np.sqrt(K) / s).astype(np.float32),
        "w1": (n((K, N)) / np.sqrt(K) / s).astype(np.float32),
        "w2": (n((K, N)) / np.sqrt(K) / s).astype(np.float32),
        "w3": (n((K, N)) / np.sqrt(K) / s).astype(np.float32),
        "gate": (np.tile(np.random.uniform(0.2, 1.0, (D, 1, V)), (1, P, 1))).astype(np.float32),
        "offs": striped(np.random.permutation(T)[:S]),
    }


def reference(x_words, x_scales, w0, w1, w2, w3, gate, offs):
    xq = unpack_weight(x_words, x_scales)[:, unstriped(offs)]
    y0 = mxq(f64(w0), 0, "e4m3").T @ xq[:, :V]
    y1 = mxq(f64(w1), 0, "e4m3").T @ xq[:, V:2 * V]
    y2 = mxq(f64(w2), 0, "e4m3").T @ xq[:, 2 * V:3 * V]
    y3 = mxq(f64(w3), 0, "e4m3").T @ xq[:, 3 * V:4 * V]
    out_0 = relu(y0 + y1 * f64(gate)[0, :1] + y2 * f64(gate)[1, :1] + y3 * f64(gate)[2, :1])
    return (out_0,) + planes(out_0)

@@ -1,0 +1,269 @@
+from contextlib import ExitStack
+
+import concourse.mybir as mybir
+from concourse.masks import make_identity
+
+K, T, S, V, D, N = 1024, 4096, 1024, 256, 3, 512
+FLOPS = 2 * K * N * S
+
+F32 = mybir.dt.float32
+BF16 = mybir.dt.bfloat16
+I32 = mybir.dt.int32
+U32 = mybir.dt.uint32
+U16 = mybir.dt.uint16
+U8 = mybir.dt.uint8
+FP8X4 = mybir.dt.float8_e4m3fn_x4
+ALU = mybir.AluOpType
+ACT = mybir.ActivationFunctionType
+
+P = 128
+PACK = 4
+K_PASS = P * PACK
+PASSES = K // K_PASS
+HALVES = V // P
+QUADS = 4
+LIST_COLS = S // 16
+HALF_N = N // 2
+
+
+def tile_picked_zrgcn_relu_po_kernel(
+    tc, x_words, x_scales, w0, w1, w2, w3, gate, offs, out_0, out_1, out_2
+):
+    nc = tc.nc
+    weights = [w0, w1, w2, w3]
+
+    with ExitStack() as ctx:
+        keep = ctx.enter_context(tc.tile_pool(name="keep", bufs=1))
+        psum = ctx.enter_context(tc.psum_pool(name="psum", bufs=1))
+
+        def tile(shape, dtype, name, tag=None):
+            return keep.tile(shape, dtype, name=name, tag=tag or name, align_bytes=64)
+
+        offsets = keep.tile([P, LIST_COLS], U16, name="offsets")
+        nc.sync.dma_start(offsets[:], offs)
+
+        table_scales = tile([P, T], U8, "table_scales")
+        nc.vector.memset(table_scales[:].bitcast(I32), 0)
+        gate_rows = tile([P, V], F32, "gate_rows")
+        nc.gpsimd.memset(gate_rows[:], 0.0)
+        nc.scalar.dma_start(gate_rows[0:D, :], gate[:, 0, :])
+        identity = tile([P, P], F32, "identity")
+        make_identity(nc, identity[:])
+
+        def load_table(o):
+            words = tile([P, T], U32, "table_words%d" % o)
+            nc.sync.dma_start(words[:].bitcast(I32), x_words[o].rearrange("p c r -> p (c r)").bitcast(I32))
+            return words
+
+        def load_weight(d, o, c0, c1):
+            raw = tile([P, PACK, c1 - c0], F32, "raw%d_%d_%d" % (d, o, c0))
+            rows = weights[d][o * K_PASS : (o + 1) * K_PASS, c0:c1]
+            nc.sync.dma_start(raw[:], rows.rearrange("(p j) c -> p j c", j=PACK))
+            return raw
+
+        def load_table_scales(o):
+            for q in range(QUADS):
+                nc.sync.dma_start(
+                    table_scales[32 * q + 4 * o : 32 * q + 4 * o + 4, :].bitcast(I32),
+                    x_scales[o, 4 * q : 4 * q + 4, :].bitcast(I32),
+                )
+
+        raws = {}
+        table0 = load_table(0)
+        load_table_scales(0)
+        raws[1, 0] = load_weight(1, 0, 0, N)
+        load_table_scales(1)
+        table1 = load_table(1)
+        raws[1, 1] = load_weight(1, 1, 0, N)
+        raws[2, 0] = load_weight(2, 0, 0, N)
+        raws[2, 1] = load_weight(2, 1, 0, N)
+        raws[3, 0] = load_weight(3, 0, 0, N)
+        raw_last = [load_weight(3, 1, u * HALF_N, (u + 1) * HALF_N) for u in range(2)]
+        raw_self0 = load_weight(0, 0, 0, N)
+        raw_self1 = [load_weight(0, 1, u * HALF_N, (u + 1) * HALF_N) for u in range(2)]
+
+        gate_bank = psum.tile([P, HALVES, P], F32, name="gate_bank", tag="self0")
+        for h in range(HALVES):
+            nc.tensor.transpose(gate_bank[:, h, :], gate_rows[:, h * P : (h + 1) * P], identity[:])
+        edges = [tile([P, HALVES, 1], F32, "edges%d" % d) for d in range(D)]
+        for d in range(D):
+            nc.scalar.activation(edges[d][:], gate_bank[:, :, d : d + 1], ACT.Copy)
+
+        picked_words = [tile([P, S], U32, "picked_words%d" % o) for o in range(PASSES)]
+        picked_scales = tile([P, S], U8, "picked_scales")
+        nc.vector.tensor_copy(picked_words[0][:], table0[:].indirect(offsets[:]))
+        nc.vector.tensor_copy(picked_scales[:], table_scales[:].indirect(offsets[:]))
+
+        def round_relation(raw, split, label):
+            width = raw.shape[2]
+            grouped = tile([P, width, PACK], BF16, "grouped" + label)
+            if split > 0:
+                nc.vector.tensor_copy(
+                    grouped[:, :split, :].rearrange("p (c i) j -> p c j i", i=4),
+                    raw[:, :, :split].rearrange("p j (c i) -> p c j i", i=4),
+                )
+            if split < width:
+                nc.scalar.copy(
+                    grouped[:, split:, :].rearrange("p (c i) j -> p c j i", i=4),
+                    raw[:, :, split:].rearrange("p j (c i) -> p c j i", i=4),
+                )
+            return grouped
+
+        def quantize(grouped, label):
+            width = grouped.shape[1]
+            codes = tile([P, width], U32, "codes" + label)
+            scales = tile([P, width], U8, "scales" + label)
+            nc.vector.quantize_mx(
+                out=codes[:].bitcast(FP8X4), scales=scales[:], in_=grouped[:].rearrange("p c j -> p (c j)")
+            )
+            return codes, scales
+
+        def multiply_relation(d, o, banks, codes, scales):
+            for h in range(HALVES):
+                cols = slice(d * V + h * P, d * V + (h + 1) * P)
+                nc.tensor.matmul_mx(
+                    out=banks[h][:],
+                    lhsT=picked_words[o][:, cols].bitcast(FP8X4),
+                    lhsT_scale=picked_scales[4 * o :, cols],
+                    rhs=codes.bitcast(FP8X4),
+                    rhs_scale=scales,
+                    start=(o == 0),
+                    stop=(o == PASSES - 1),
+                )
+
+        def relation_banks(label, first, width):
+            return [psum.tile([P, width], F32, name="%s%d" % (label, h), tag="rel%d" % (first + h)) for h in range(HALVES)]
+
+        def dealt(bank):
+            return bank[:].rearrange("v (m t) -> v t m", t=PACK)
+
+        def gated_sum(out, bank, edge, earlier):
+            nc.vector.scalar_tensor_tensor(out, dealt(bank), edge, earlier, ALU.mult, ALU.add)
+
+        def relation_pass(d, o, banks, grouped):
+            codes, scales = quantize(grouped, "%d_%d" % (d, o))
+            multiply_relation(d, o, banks, codes[:], scales[:])
+
+        banks1 = relation_banks("one", 0, N)
+        banks2 = relation_banks("two", 2, N)
+        relation_pass(1, 0, banks1, round_relation(raws[1, 0], 0, "1_0"))
+        for u in range(2):
+            entries = slice(u * (S // 2), (u + 1) * (S // 2))
+            list_cols = slice(u * (LIST_COLS // 2), (u + 1) * (LIST_COLS // 2))
+            nc.vector.tensor_copy(picked_words[1][:, entries], table1[:].indirect(offsets[:, list_cols]))
+        relation_pass(1, 1, banks1, round_relation(raws[1, 1], 192, "1_1"))
+
+        grouped = round_relation(raws[2, 0], 224, "2_0")
+        sums1 = [tile([P, PACK, P], F32, "sums1_%d" % h) for h in range(HALVES)]
+        for h in range(HALVES):
+            nc.scalar.activation(sums1[h][:], dealt(banks1[h]), ACT.Copy, scale=edges[0][:, h, :])
+        relation_pass(2, 0, banks2, grouped)
+        relation_pass(2, 1, banks2, round_relation(raws[2, 1], 320, "2_1"))
+
+        grouped = round_relation(raws[3, 0], 192, "3_0")
+        sums2 = [tile([P, PACK, P], F32, "sums2_%d" % h) for h in range(HALVES)]
+        for h in range(HALVES):
+            gated_sum(sums2[h][:], banks2[h], edges[1][:, h, :], sums1[h][:])
+        codes, scales = quantize(grouped, "3_0")
+        last_banks = [relation_banks("three%d_" % u, 2 * u, HALF_N) for u in range(2)]
+        for u in range(2):
+            cols = slice(u * HALF_N, (u + 1) * HALF_N)
+            multiply_relation(3, 0, last_banks[u], codes[:, cols], scales[:, cols])
+        last_grouped = [round_relation(raw_last[u], u * HALF_N, "3_1_%d" % u) for u in range(2)]
+        for u in range(2):
+            codes, scales = quantize(last_grouped[u], "3_1_%d" % u)
+            multiply_relation(3, 1, last_banks[u], codes[:], scales[:])
+        sums = [tile([P, PACK, P], F32, "sums3_%d" % h) for h in range(HALVES)]
+        for u in range(2):
+            part = slice(u * (P // 2), (u + 1) * (P // 2))
+            for h in range(HALVES):
+                gated_sum(sums[h][:, :, part], last_banks[u][h], edges[2][:, h, :], sums2[h][:, :, part])
+        turned = [psum.tile([P, 2, V], F32, name="turned%d" % u, tag="rel%d" % u) for u in range(2)]
+        for h in range(HALVES):
+            for t in range(PACK):
+                nc.tensor.transpose(turned[t // 2][:, t % 2, h * P : (h + 1) * P], sums[h][:, t, :], identity[:])
+
+        self_codes = [tile([P, PACK, P], U32, "self_codes%d" % o) for o in range(PASSES)]
+        self_scales = [tile([P, PACK, P], U8, "self_scales%d" % o) for o in range(PASSES)]
+        self_banks = [psum.tile([P, V], F32, name="self_bank%d" % t, tag="self%d" % t) for t in range(PACK)]
+
+        def round_self(copy, raw, pair, u, m0):
+            width = raw.shape[2] // PACK
+            by_tile = raw[:].rearrange("p j (m t) -> p m j t", t=PACK)
+            copy(pair[:, :, m0 : m0 + width, :].rearrange("p t m j -> p m j t"), by_tile[:, :, :, 2 * u : 2 * u + 2])
+
+        def multiply_self(o, t):
+            nc.tensor.matmul_mx(
+                out=self_banks[t][:],
+                lhsT=self_codes[o][:, t, :].bitcast(FP8X4),
+                lhsT_scale=self_scales[o][:, t, :],
+                rhs=picked_words[o][:, 0:V].bitcast(FP8X4),
+                rhs_scale=picked_scales[4 * o :, 0:V],
+                start=(o == 0),
+                stop=(o == PASSES - 1),
+            )
+
+        pairs = [tile([P, 2, P, PACK], BF16, "self_grouped0_%d" % u) for u in range(2)]
+        round_self(nc.vector.tensor_copy, raw_self0, pairs[0], 0, 0)
+        round_self(nc.scalar.copy, raw_self0, pairs[1], 1, 0)
+        for u in (1, 0):
+            nc.vector.quantize_mx(
+                out=self_codes[0][:, 2 * u : 2 * u + 2, :].rearrange("p t m -> p (t m)").bitcast(FP8X4),
+                scales=self_scales[0][:, 2 * u : 2 * u + 2, :].rearrange("p t m -> p (t m)"),
+                in_=pairs[u][:].rearrange("p t m j -> p (t m j)"),
+            )
+            for t in (2 * u, 2 * u + 1):
+                multiply_self(0, t)
+
+        pairs = [tile([P, 2, P, PACK], BF16, "self_grouped1_%d" % u) for u in range(2)]
+        for u in range(2):
+            round_self(nc.scalar.copy, raw_self1[0], pairs[u], u, 0)
+        round_self(nc.vector.tensor_copy, raw_self1[1], pairs[0], 0, P // 2)
+        round_self(nc.scalar.copy, raw_self1[1], pairs[1], 1, P // 2)
+        for t in range(PACK):
+            nc.vector.quantize_mx(
+                out=self_codes[1][:, t, :].bitcast(FP8X4),
+                scales=self_scales[1][:, t, :],
+                in_=pairs[t // 2][:, t % 2].rearrange("p m j -> p (m j)"),
+            )
+            multiply_self(1, t)
+
+        neighbours = tile([P, PACK, V], F32, "neighbours")
+        for t in range(PACK):
+            nc.scalar.copy(neighbours[:, t, :], turned[t // 2][:, t % 2, :])
+
+        total = tile([P, PACK, V], F32, "total")
+        for t in range(PACK - 1):
+            nc.vector.tensor_tensor(total[:, t, :], self_banks[t][:], neighbours[:, t, :], ALU.add)
+        t = PACK - 1
+        for h in range(HALVES):
+            cols = slice(h * P, (h + 1) * P)
+            nc.vector.tensor_tensor(total[:, t, cols], self_banks[t][:, cols], neighbours[:, t, cols], ALU.add)
+
+        out_rows = out_0.rearrange("(p t) v -> p t v", t=PACK)
+        for u in range(2):
+            result = tile([P, 2, V], F32, "result%d" % u)
+            nc.scalar.activation(result[:], total[:, 2 * u : 2 * u + 2, :], ACT.Relu)
+            nc.sync.dma_start(out_rows[:, 2 * u : 2 * u + 2, :], result[:])
+
+        rounded = [tile([P, P, PACK], BF16, "rounded%d" % h) for h in range(HALVES)]
+        for h in range(HALVES):
+            nc.vector.tensor_scalar_max(
+                rounded[h][:].rearrange("p (c i) t -> p c t i", i=4),
+                total[:, :, h * P : (h + 1) * P].rearrange("p t (c i) -> p c t i", i=4),
+                0.0,
+            )
+        out_codes = tile([P, V], U32, "out_codes")
+        out_scales = tile([P, V], U8, "out_scales")
+        words_out = out_1[0].rearrange("p c r -> p (c r)").bitcast(I32)
+        for h in range(HALVES):
+            cols = slice(h * P, (h + 1) * P)
+            nc.vector.quantize_mx(
+                out=out_codes[:, cols].bitcast(FP8X4),
+                scales=out_scales[:, cols],
+                in_=rounded[h][:].rearrange("p c t -> p (c t)"),
+            )
+            nc.sync.dma_start(words_out[:, cols], out_codes[:, cols].bitcast(I32))
+        for q in range(QUADS):
+            queue = nc.sync if q < 2 else nc.scalar
+            queue.dma_start(out_2[0, 4 * q : 4 * q + 4, :].bitcast(I32), out_scales[32 * q : 32 * q + 4, :].bitcast(I32))

@@ -46,7 +46,12 @@ def tile_picked_zrgcn_relu_po_kernel(
         nc.vector.memset(table_scales[:].bitcast(I32), 0)
         gate_rows = tile([P, V], F32, "gate_rows")
         nc.gpsimd.memset(gate_rows[:], 0.0)
-        nc.scalar.dma_start(gate_rows[0:D, :], gate[:, 0, :])
+        nc.gpsimd.dma_start(
+            table_scales[0:P:4, :].bitcast(I32), x_scales.rearrange("o q c -> (o q) c").bitcast(I32)
+        )
+        nc.gpsimd.dma_start(gate_rows[0:D, :], gate[:, 0, :])
+        picked_scales = tile([P, S], U8, "picked_scales")
+        nc.vector.memset(picked_scales[:].bitcast(I32), 0)
         identity = tile([P, P], F32, "identity")
         make_identity(nc, identity[:])
 
@@ -61,18 +66,9 @@ def tile_picked_zrgcn_relu_po_kernel(
             nc.sync.dma_start(raw[:], rows.rearrange("(p j) c -> p j c", j=PACK))
             return raw
 
-        def load_table_scales(o):
-            for q in range(QUADS):
-                nc.sync.dma_start(
-                    table_scales[32 * q + 4 * o : 32 * q + 4 * o + 4, :].bitcast(I32),
-                    x_scales[o, 4 * q : 4 * q + 4, :].bitcast(I32),
-                )
-
         raws = {}
         table0 = load_table(0)
-        load_table_scales(0)
         raws[1, 0] = load_weight(1, 0, 0, N)
-        load_table_scales(1)
         table1 = load_table(1)
         raws[1, 1] = load_weight(1, 1, 0, N)
         raws[2, 0] = load_weight(2, 0, 0, N)
@@ -90,9 +86,16 @@ def tile_picked_zrgcn_relu_po_kernel(
             nc.scalar.activation(edges[d][:], gate_bank[:, :, d : d + 1], ACT.Copy)
 
         picked_words = [tile([P, S], U32, "picked_words%d" % o) for o in range(PASSES)]
-        picked_scales = tile([P, S], U8, "picked_scales")
+        spread_scales = tile([P, S], U8, "spread_scales")
+        nc.vector.tensor_copy(spread_scales[:], table_scales[:].indirect(offsets[:]))
+        for o in range(PASSES):
+            for r in range(4):
+                first = 64 * o + 4 * r
+                nc.gpsimd.dma_start(
+                    picked_scales[4 * o + r : P : 32, :].bitcast(I32),
+                    spread_scales[first : first + 49 : 16, :].bitcast(I32),
+                )
         nc.vector.tensor_copy(picked_words[0][:], table0[:].indirect(offsets[:]))
-        nc.vector.tensor_copy(picked_scales[:], table_scales[:].indirect(offsets[:]))
 
         def round_relation(raw, split, label):
             width = raw.shape[2]
@@ -174,10 +177,21 @@ def tile_picked_zrgcn_relu_po_kernel(
             codes, scales = quantize(last_grouped[u], "3_1_%d" % u)
             multiply_relation(3, 1, last_banks[u], codes[:], scales[:])
         sums = [tile([P, PACK, P], F32, "sums3_%d" % h) for h in range(HALVES)]
-        for u in range(2):
+        def round_self(copy, raw, pair, u, m0):
+            width = raw.shape[2] // PACK
+            by_tile = raw[:].rearrange("p j (m t) -> p m j t", t=PACK)
+            copy(pair[:, :, m0 : m0 + width, :].rearrange("p t m j -> p m j t"), by_tile[:, :, :, 2 * u : 2 * u + 2])
+
+        def last_sums(u):
             part = slice(u * (P // 2), (u + 1) * (P // 2))
             for h in range(HALVES):
                 gated_sum(sums[h][:, :, part], last_banks[u][h], edges[2][:, h, :], sums2[h][:, :, part])
+
+        pairs = [tile([P, 2, P, PACK], BF16, "self_grouped0_%d" % u) for u in range(2)]
+        last_sums(0)
+        round_self(nc.vector.tensor_copy, raw_self0, pairs[0], 0, 0)
+        round_self(nc.scalar.copy, raw_self0, pairs[1], 1, 0)
+        last_sums(1)
         turned = [psum.tile([P, 2, V], F32, name="turned%d" % u, tag="rel%d" % u) for u in range(2)]
         for h in range(HALVES):
             for t in range(PACK):
@@ -186,11 +200,6 @@ def tile_picked_zrgcn_relu_po_kernel(
         self_codes = [tile([P, PACK, P], U32, "self_codes%d" % o) for o in range(PASSES)]
         self_scales = [tile([P, PACK, P], U8, "self_scales%d" % o) for o in range(PASSES)]
         self_banks = [psum.tile([P, V], F32, name="self_bank%d" % t, tag="self%d" % t) for t in range(PACK)]
-
-        def round_self(copy, raw, pair, u, m0):
-            width = raw.shape[2] // PACK
-            by_tile = raw[:].rearrange("p j (m t) -> p m j t", t=PACK)
-            copy(pair[:, :, m0 : m0 + width, :].rearrange("p t m j -> p m j t"), by_tile[:, :, :, 2 * u : 2 * u + 2])
 
         def multiply_self(o, t):
             nc.tensor.matmul_mx(
@@ -203,10 +212,7 @@ def tile_picked_zrgcn_relu_po_kernel(
                 stop=(o == PASSES - 1),
             )
 
-        pairs = [tile([P, 2, P, PACK], BF16, "self_grouped0_%d" % u) for u in range(2)]
-        round_self(nc.vector.tensor_copy, raw_self0, pairs[0], 0, 0)
-        round_self(nc.scalar.copy, raw_self0, pairs[1], 1, 0)
-        for u in (1, 0):
+        for u in range(2):
             nc.vector.quantize_mx(
                 out=self_codes[0][:, 2 * u : 2 * u + 2, :].rearrange("p t m -> p (t m)").bitcast(FP8X4),
                 scales=self_scales[0][:, 2 * u : 2 * u + 2, :].rearrange("p t m -> p (t m)"),

@@ -46,37 +46,31 @@ def tile_picked_zrgcn_relu_po_kernel(
         nc.vector.memset(table_scales[:].bitcast(I32), 0)
         gate_rows = tile([P, V], F32, "gate_rows")
         nc.gpsimd.memset(gate_rows[:], 0.0)
-        nc.gpsimd.dma_start(
-            table_scales[0:P:4, :].bitcast(I32), x_scales.rearrange("o q c -> (o q) c").bitcast(I32)
-        )
-        nc.gpsimd.dma_start(gate_rows[0:D, :], gate[:, 0, :])
         picked_scales = tile([P, S], U8, "picked_scales")
         nc.vector.memset(picked_scales[:].bitcast(I32), 0)
         identity = tile([P, P], F32, "identity")
         make_identity(nc, identity[:])
 
-        def load_table(o):
-            words = tile([P, T], U32, "table_words%d" % o)
-            nc.sync.dma_start(words[:].bitcast(I32), x_words[o].rearrange("p c r -> p (c r)").bitcast(I32))
-            return words
+        def load_table(words, o, c0, c1):
+            rows = x_words[o].rearrange("p c r -> p (c r)").bitcast(I32)
+            nc.sync.dma_start(words[:, c0:c1].bitcast(I32), rows[:, c0:c1])
 
-        def load_weight(d, o, c0, c1):
-            raw = tile([P, PACK, c1 - c0], F32, "raw%d_%d_%d" % (d, o, c0))
+        def load_weight(d, o, c0, c1, tag=None):
+            raw = tile([P, PACK, c1 - c0], F32, "raw%d_%d_%d" % (d, o, c0), tag)
             rows = weights[d][o * K_PASS : (o + 1) * K_PASS, c0:c1]
             nc.sync.dma_start(raw[:], rows.rearrange("(p j) c -> p j c", j=PACK))
             return raw
 
         raws = {}
-        table0 = load_table(0)
+        table0 = tile([P, T], U32, "table0", "table")
+        load_table(table0, 0, 0, T // 2)
+        nc.scalar.dma_start(gate_rows[0:D, :], gate[:, 0, :])
+        nc.sync.dma_start(
+            table_scales[0:P:4, :].bitcast(I32), x_scales.rearrange("o q c -> (o q) c").bitcast(I32)
+        )
+        load_table(table0, 0, T // 2, T)
         raws[1, 0] = load_weight(1, 0, 0, N)
-        table1 = load_table(1)
         raws[1, 1] = load_weight(1, 1, 0, N)
-        raws[2, 0] = load_weight(2, 0, 0, N)
-        raws[2, 1] = load_weight(2, 1, 0, N)
-        raws[3, 0] = load_weight(3, 0, 0, N)
-        raw_last = [load_weight(3, 1, u * HALF_N, (u + 1) * HALF_N) for u in range(2)]
-        raw_self0 = load_weight(0, 0, 0, N)
-        raw_self1 = [load_weight(0, 1, u * HALF_N, (u + 1) * HALF_N) for u in range(2)]
 
         gate_bank = psum.tile([P, HALVES, P], F32, name="gate_bank", tag="self0")
         for h in range(HALVES):
@@ -88,14 +82,20 @@ def tile_picked_zrgcn_relu_po_kernel(
         picked_words = [tile([P, S], U32, "picked_words%d" % o) for o in range(PASSES)]
         spread_scales = tile([P, S], U8, "spread_scales")
         nc.vector.tensor_copy(spread_scales[:], table_scales[:].indirect(offsets[:]))
-        for o in range(PASSES):
-            for r in range(4):
-                first = 64 * o + 4 * r
-                nc.gpsimd.dma_start(
-                    picked_scales[4 * o + r : P : 32, :].bitcast(I32),
-                    spread_scales[first : first + 49 : 16, :].bitcast(I32),
-                )
+
+        def place_scale_rows(o, r):
+            first = 64 * o + 4 * r
+            nc.scalar.dma_start(
+                picked_scales[4 * o + r : P : 32, :].bitcast(I32),
+                spread_scales[first : first + 49 : 16, :].bitcast(I32),
+            )
+
+        scale_rows = [(o, r) for o in range(PASSES) for r in range(4)]
+        for o, r in scale_rows:
+            place_scale_rows(o, r)
         nc.vector.tensor_copy(picked_words[0][:], table0[:].indirect(offsets[:]))
+        table1 = tile([P, T], U32, "table1", "table")
+        load_table(table1, 1, 0, T)
 
         def round_relation(raw, split, label):
             width = raw.shape[2]
@@ -149,51 +149,45 @@ def tile_picked_zrgcn_relu_po_kernel(
 
         banks1 = relation_banks("one", 0, N)
         banks2 = relation_banks("two", 2, N)
-        relation_pass(1, 0, banks1, round_relation(raws[1, 0], 0, "1_0"))
+        relation_pass(1, 0, banks1, round_relation(raws[1, 0], N, "1_0"))
+        codes, scales = quantize(round_relation(raws[1, 1], 256, "1_1"), "1_1")
+        raws[2, 0] = load_weight(2, 0, 0, N, "raw1_1_0")
+        for d, o in [(2, 1), (3, 0), (3, 1), (0, 0), (0, 1)]:
+            raws[d, o] = load_weight(d, o, 0, N)
         for u in range(2):
             entries = slice(u * (S // 2), (u + 1) * (S // 2))
             list_cols = slice(u * (LIST_COLS // 2), (u + 1) * (LIST_COLS // 2))
             nc.vector.tensor_copy(picked_words[1][:, entries], table1[:].indirect(offsets[:, list_cols]))
-        relation_pass(1, 1, banks1, round_relation(raws[1, 1], 192, "1_1"))
+        multiply_relation(1, 1, banks1, codes[:], scales[:])
 
-        grouped = round_relation(raws[2, 0], 224, "2_0")
+        grouped = round_relation(raws[2, 0], 192, "2_0")
         sums1 = [tile([P, PACK, P], F32, "sums1_%d" % h) for h in range(HALVES)]
-        for h in range(HALVES):
-            nc.scalar.activation(sums1[h][:], dealt(banks1[h]), ACT.Copy, scale=edges[0][:, h, :])
+        nc.scalar.activation(sums1[0][:], dealt(banks1[0]), ACT.Copy, scale=edges[0][:, 0, :])
+        nc.vector.tensor_scalar_mul(sums1[1][:], dealt(banks1[1]), edges[0][:, 1, :])
         relation_pass(2, 0, banks2, grouped)
-        relation_pass(2, 1, banks2, round_relation(raws[2, 1], 320, "2_1"))
+        relation_pass(2, 1, banks2, round_relation(raws[2, 1], 256, "2_1"))
 
-        grouped = round_relation(raws[3, 0], 192, "3_0")
+        grouped = round_relation(raws[3, 0], 128, "3_0")
         sums2 = [tile([P, PACK, P], F32, "sums2_%d" % h) for h in range(HALVES)]
         for h in range(HALVES):
             gated_sum(sums2[h][:], banks2[h], edges[1][:, h, :], sums1[h][:])
-        codes, scales = quantize(grouped, "3_0")
-        last_banks = [relation_banks("three%d_" % u, 2 * u, HALF_N) for u in range(2)]
-        for u in range(2):
-            cols = slice(u * HALF_N, (u + 1) * HALF_N)
-            multiply_relation(3, 0, last_banks[u], codes[:, cols], scales[:, cols])
-        last_grouped = [round_relation(raw_last[u], u * HALF_N, "3_1_%d" % u) for u in range(2)]
-        for u in range(2):
-            codes, scales = quantize(last_grouped[u], "3_1_%d" % u)
-            multiply_relation(3, 1, last_banks[u], codes[:], scales[:])
-        sums = [tile([P, PACK, P], F32, "sums3_%d" % h) for h in range(HALVES)]
-        def round_self(copy, raw, pair, u, m0):
-            width = raw.shape[2] // PACK
-            by_tile = raw[:].rearrange("p j (m t) -> p m j t", t=PACK)
-            copy(pair[:, :, m0 : m0 + width, :].rearrange("p t m j -> p m j t"), by_tile[:, :, :, 2 * u : 2 * u + 2])
+        banks3 = relation_banks("three", 0, N)
+        relation_pass(3, 0, banks3, grouped)
+        relation_pass(3, 1, banks3, round_relation(raws[3, 1], 256, "3_1"))
 
-        def last_sums(u):
-            part = slice(u * (P // 2), (u + 1) * (P // 2))
-            for h in range(HALVES):
-                gated_sum(sums[h][:, :, part], last_banks[u][h], edges[2][:, h, :], sums2[h][:, :, part])
+        def round_self(copy, o, pair, u, m0, m1):
+            by_tile = raws[0, o][:].rearrange("p j (m t) -> p m j t", t=PACK)
+            copy(pair[:, :, m0:m1, :].rearrange("p t m j -> p m j t"), by_tile[:, m0:m1, :, 2 * u : 2 * u + 2])
 
         pairs = [tile([P, 2, P, PACK], BF16, "self_grouped0_%d" % u) for u in range(2)]
-        last_sums(0)
-        round_self(nc.vector.tensor_copy, raw_self0, pairs[0], 0, 0)
-        round_self(nc.scalar.copy, raw_self0, pairs[1], 1, 0)
-        last_sums(1)
-        turned = [psum.tile([P, 2, V], F32, name="turned%d" % u, tag="rel%d" % u) for u in range(2)]
+        round_self(nc.vector.tensor_copy, 0, pairs[0], 0, 0, P // 2)
+        round_self(nc.scalar.copy, 0, pairs[0], 0, P // 2, P)
+        round_self(nc.scalar.copy, 0, pairs[1], 1, 0, P)
+
+        sums = [tile([P, PACK, P], F32, "sums3_%d" % h) for h in range(HALVES)]
+        turned = [psum.tile([P, 2, V], F32, name="turned%d" % u, tag="rel%d" % (2 + u)) for u in range(2)]
         for h in range(HALVES):
+            gated_sum(sums[h][:], banks3[h], edges[2][:, h, :], sums2[h][:])
             for t in range(PACK):
                 nc.tensor.transpose(turned[t // 2][:, t % 2, h * P : (h + 1) * P], sums[h][:, t, :], identity[:])
 
@@ -222,10 +216,8 @@ def tile_picked_zrgcn_relu_po_kernel(
                 multiply_self(0, t)
 
         pairs = [tile([P, 2, P, PACK], BF16, "self_grouped1_%d" % u) for u in range(2)]
-        for u in range(2):
-            round_self(nc.scalar.copy, raw_self1[0], pairs[u], u, 0)
-        round_self(nc.vector.tensor_copy, raw_self1[1], pairs[0], 0, P // 2)
-        round_self(nc.scalar.copy, raw_self1[1], pairs[1], 1, P // 2)
+        round_self(nc.vector.tensor_copy, 1, pairs[0], 0, 0, P)
+        round_self(nc.scalar.copy, 1, pairs[1], 1, 0, P)
         for t in range(PACK):
             nc.vector.quantize_mx(
                 out=self_codes[1][:, t, :].bitcast(FP8X4),

@@ -171,25 +171,37 @@ def tile_picked_zrgcn_relu_po_kernel(
         sums2 = [tile([P, PACK, P], F32, "sums2_%d" % h) for h in range(HALVES)]
         for h in range(HALVES):
             gated_sum(sums2[h][:], banks2[h], edges[1][:, h, :], sums1[h][:])
+        turned = [psum.tile([P, 2, V], F32, name="turned%d" % u, tag="rel%d" % (2 + u)) for u in range(2)]
+
+        def turn(terms, first):
+            for u in range(2):
+                for h in range(HALVES):
+                    for e in range(2):
+                        nc.tensor.matmul(
+                            turned[u][:, e, h * P : (h + 1) * P],
+                            terms[h][:, 2 * u + e, :],
+                            identity[:],
+                            is_transpose=True,
+                            start=(first and h == 0 and e == 0),
+                            stop=(not first and h == HALVES - 1 and e == 1),
+                        )
+
+        turn(sums2, True)
         banks3 = relation_banks("three", 0, N)
         relation_pass(3, 0, banks3, grouped)
-        relation_pass(3, 1, banks3, round_relation(raws[3, 1], 256, "3_1"))
+        relation_pass(3, 1, banks3, round_relation(raws[3, 1], 192, "3_1"))
 
         def round_self(copy, o, pair, u, m0, m1):
             by_tile = raws[0, o][:].rearrange("p j (m t) -> p m j t", t=PACK)
             copy(pair[:, :, m0:m1, :].rearrange("p t m j -> p m j t"), by_tile[:, m0:m1, :, 2 * u : 2 * u + 2])
 
         pairs = [tile([P, 2, P, PACK], BF16, "self_grouped0_%d" % u) for u in range(2)]
-        round_self(nc.vector.tensor_copy, 0, pairs[0], 0, 0, P // 2)
-        round_self(nc.scalar.copy, 0, pairs[0], 0, P // 2, P)
+        round_self(nc.vector.tensor_copy, 0, pairs[0], 0, 0, P)
         round_self(nc.scalar.copy, 0, pairs[1], 1, 0, P)
 
-        sums = [tile([P, PACK, P], F32, "sums3_%d" % h) for h in range(HALVES)]
-        turned = [psum.tile([P, 2, V], F32, name="turned%d" % u, tag="rel%d" % (2 + u)) for u in range(2)]
+        terms3 = [tile([P, PACK, P], F32, "terms3_%d" % h) for h in range(HALVES)]
         for h in range(HALVES):
-            gated_sum(sums[h][:], banks3[h], edges[2][:, h, :], sums2[h][:])
-            for t in range(PACK):
-                nc.tensor.transpose(turned[t // 2][:, t % 2, h * P : (h + 1) * P], sums[h][:, t, :], identity[:])
+            nc.scalar.activation(terms3[h][:], dealt(banks3[h]), ACT.Copy, scale=edges[2][:, h, :])
 
         self_codes = [tile([P, PACK, P], U32, "self_codes%d" % o) for o in range(PASSES)]
         self_scales = [tile([P, PACK, P], U8, "self_scales%d" % o) for o in range(PASSES)]
@@ -206,7 +218,7 @@ def tile_picked_zrgcn_relu_po_kernel(
                 stop=(o == PASSES - 1),
             )
 
-        for u in range(2):
+        for u in (1, 0):
             nc.vector.quantize_mx(
                 out=self_codes[0][:, 2 * u : 2 * u + 2, :].rearrange("p t m -> p (t m)").bitcast(FP8X4),
                 scales=self_scales[0][:, 2 * u : 2 * u + 2, :].rearrange("p t m -> p (t m)"),
@@ -215,9 +227,11 @@ def tile_picked_zrgcn_relu_po_kernel(
             for t in (2 * u, 2 * u + 1):
                 multiply_self(0, t)
 
+        turn(terms3, False)
         pairs = [tile([P, 2, P, PACK], BF16, "self_grouped1_%d" % u) for u in range(2)]
         round_self(nc.vector.tensor_copy, 1, pairs[0], 0, 0, P)
-        round_self(nc.scalar.copy, 1, pairs[1], 1, 0, P)
+        round_self(nc.scalar.copy, 1, pairs[1], 1, P // 2, P)
+        round_self(nc.vector.tensor_copy, 1, pairs[1], 1, 0, P // 2)
         for t in range(PACK):
             nc.vector.quantize_mx(
                 out=self_codes[1][:, t, :].bitcast(FP8X4),

@@ -23,7 +23,6 @@ PASSES = K // K_PASS
 HALVES = V // P
 QUADS = 4
 LIST_COLS = S // 16
-HALF_N = N // 2
 
 
 def tile_picked_zrgcn_relu_po_kernel(
@@ -40,14 +39,10 @@ def tile_picked_zrgcn_relu_po_kernel(
             return keep.tile(shape, dtype, name=name, tag=tag or name, align_bytes=64)
 
         offsets = keep.tile([P, LIST_COLS], U16, name="offsets")
-        nc.sync.dma_start(offsets[:], offs)
-
         table_scales = tile([P, T], U8, "table_scales")
         nc.vector.memset(table_scales[:].bitcast(I32), 0)
         gate_rows = tile([P, V], F32, "gate_rows")
         nc.gpsimd.memset(gate_rows[:], 0.0)
-        picked_scales = tile([P, S], U8, "picked_scales")
-        nc.vector.memset(picked_scales[:].bitcast(I32), 0)
         identity = tile([P, P], F32, "identity")
         make_identity(nc, identity[:])
 
@@ -55,24 +50,24 @@ def tile_picked_zrgcn_relu_po_kernel(
             rows = x_words[o].rearrange("p c r -> p (c r)").bitcast(I32)
             nc.sync.dma_start(words[:, c0:c1].bitcast(I32), rows[:, c0:c1])
 
-        def load_weight(d, o, c0, c1, tag=None):
-            raw = tile([P, PACK, c1 - c0], F32, "raw%d_%d_%d" % (d, o, c0), tag)
-            rows = weights[d][o * K_PASS : (o + 1) * K_PASS, c0:c1]
+        def load_weight(d, o):
+            raw = tile([P, PACK, N], F32, "raw%d_%d" % (d, o))
+            rows = weights[d][o * K_PASS : (o + 1) * K_PASS, :]
             nc.sync.dma_start(raw[:], rows.rearrange("(p j) c -> p j c", j=PACK))
             return raw
 
         raws = {}
-        table0 = tile([P, T], U32, "table0", "table")
-        load_table(table0, 0, 0, T // 2)
+        tables = [tile([P, T], U32, "table%d" % o) for o in range(PASSES)]
+        load_table(tables[0], 0, 0, T // 2)
+        nc.sync.dma_start(offsets[:], offs)
         nc.scalar.dma_start(gate_rows[0:D, :], gate[:, 0, :])
-        nc.sync.dma_start(
-            table_scales[0:P:4, :].bitcast(I32), x_scales.rearrange("o q c -> (o q) c").bitcast(I32)
-        )
-        load_table(table0, 0, T // 2, T)
-        raws[1, 0] = load_weight(1, 0, 0, N)
-        raws[1, 1] = load_weight(1, 1, 0, N)
+        for o in range(PASSES):
+            nc.sync.dma_start(table_scales[4 * o : P : 8, :].bitcast(I32), x_scales[o].bitcast(I32))
+        load_table(tables[0], 0, T // 2, T)
+        raws[1, 0] = load_weight(1, 0)
+        load_table(tables[1], 1, 0, T)
 
-        gate_bank = psum.tile([P, HALVES, P], F32, name="gate_bank", tag="self0")
+        gate_bank = psum.tile([P, HALVES, P], F32, name="gate_bank", tag="bank6")
         for h in range(HALVES):
             nc.tensor.transpose(gate_bank[:, h, :], gate_rows[:, h * P : (h + 1) * P], identity[:])
         edges = [tile([P, HALVES, 1], F32, "edges%d" % d) for d in range(D)]
@@ -82,165 +77,144 @@ def tile_picked_zrgcn_relu_po_kernel(
         picked_words = [tile([P, S], U32, "picked_words%d" % o) for o in range(PASSES)]
         spread_scales = tile([P, S], U8, "spread_scales")
         nc.vector.tensor_copy(spread_scales[:], table_scales[:].indirect(offsets[:]))
-
-        def place_scale_rows(o, r):
-            first = 64 * o + 4 * r
-            nc.scalar.dma_start(
-                picked_scales[4 * o + r : P : 32, :].bitcast(I32),
-                spread_scales[first : first + 49 : 16, :].bitcast(I32),
-            )
-
-        scale_rows = [(o, r) for o in range(PASSES) for r in range(4)]
-        for o, r in scale_rows:
-            place_scale_rows(o, r)
-        nc.vector.tensor_copy(picked_words[0][:], table0[:].indirect(offsets[:]))
-        table1 = tile([P, T], U32, "table1", "table")
-        load_table(table1, 1, 0, T)
-
-        def round_relation(raw, split, label):
-            width = raw.shape[2]
-            grouped = tile([P, width, PACK], BF16, "grouped" + label)
-            if split > 0:
-                nc.vector.tensor_copy(
-                    grouped[:, :split, :].rearrange("p (c i) j -> p c j i", i=4),
-                    raw[:, :, :split].rearrange("p j (c i) -> p c j i", i=4),
+        picked_scales = tile([P, S], U8, "picked_scales")
+        nc.vector.tensor_copy(picked_scales[:].bitcast(I32), spread_scales[:].bitcast(I32))
+        for o in range(PASSES):
+            for r in range(1, 4):
+                nc.scalar.dma_start(
+                    picked_scales[4 * o + r : P : 32, :].bitcast(I32),
+                    spread_scales[4 * o + 8 * r : P : 32, :].bitcast(I32),
                 )
-            if split < width:
-                nc.scalar.copy(
-                    grouped[:, split:, :].rearrange("p (c i) j -> p c j i", i=4),
-                    raw[:, :, split:].rearrange("p j (c i) -> p c j i", i=4),
+        nc.vector.tensor_copy(picked_words[0][:], tables[0][:].indirect(offsets[:]))
+        for d, o in [(1, 1), (2, 0), (2, 1), (3, 0), (3, 1), (0, 0), (0, 1)]:
+            raws[d, o] = load_weight(d, o)
+
+        def round_relation(d, o, split):
+            raw = raws[d, o]
+            grouped = tile([P, N, PACK], BF16, "grouped%d_%d" % (d, o))
+            for copy, c0, c1 in ((nc.vector.tensor_copy, 0, split), (nc.scalar.copy, split, N)):
+                copy(
+                    grouped[:, c0:c1, :].rearrange("p (c i) j -> p c j i", i=4),
+                    raw[:, :, c0:c1].rearrange("p j (c i) -> p c j i", i=4),
                 )
             return grouped
 
-        def quantize(grouped, label):
-            width = grouped.shape[1]
-            codes = tile([P, width], U32, "codes" + label)
-            scales = tile([P, width], U8, "scales" + label)
+        def relation_pass(d, o, banks, grouped):
+            codes = tile([P, N], U32, "codes%d_%d" % (d, o))
+            scales = tile([P, N], U8, "scales%d_%d" % (d, o))
             nc.vector.quantize_mx(
                 out=codes[:].bitcast(FP8X4), scales=scales[:], in_=grouped[:].rearrange("p c j -> p (c j)")
             )
-            return codes, scales
-
-        def multiply_relation(d, o, banks, codes, scales):
             for h in range(HALVES):
                 cols = slice(d * V + h * P, d * V + (h + 1) * P)
                 nc.tensor.matmul_mx(
                     out=banks[h][:],
                     lhsT=picked_words[o][:, cols].bitcast(FP8X4),
                     lhsT_scale=picked_scales[4 * o :, cols],
-                    rhs=codes.bitcast(FP8X4),
-                    rhs_scale=scales,
+                    rhs=codes[:].bitcast(FP8X4),
+                    rhs_scale=scales[:],
                     start=(o == 0),
                     stop=(o == PASSES - 1),
                 )
+            return codes
 
-        def relation_banks(label, first, width):
-            return [psum.tile([P, width], F32, name="%s%d" % (label, h), tag="rel%d" % (first + h)) for h in range(HALVES)]
+        def relation_banks(label, first):
+            return [psum.tile([P, N], F32, name="%s%d" % (label, h), tag="bank%d" % (first + h)) for h in range(HALVES)]
 
         def dealt(bank):
             return bank[:].rearrange("v (m t) -> v t m", t=PACK)
 
-        def gated_sum(out, bank, edge, earlier):
-            nc.vector.scalar_tensor_tensor(out, dealt(bank), edge, earlier, ALU.mult, ALU.add)
+        def spent_columns(raw):
+            return [raw[:, :, N - (h + 1) * P : N - h * P] for h in range(HALVES)]
 
-        def relation_pass(d, o, banks, grouped):
-            codes, scales = quantize(grouped, "%d_%d" % (d, o))
-            multiply_relation(d, o, banks, codes[:], scales[:])
+        def gate_on_scalar(d, banks, terms, h):
+            nc.scalar.activation(terms[h], dealt(banks[h]), ACT.Copy, scale=edges[d - 1][:, h, :])
 
-        banks1 = relation_banks("one", 0, N)
-        banks2 = relation_banks("two", 2, N)
-        relation_pass(1, 0, banks1, round_relation(raws[1, 0], N, "1_0"))
-        codes, scales = quantize(round_relation(raws[1, 1], 256, "1_1"), "1_1")
-        raws[2, 0] = load_weight(2, 0, 0, N, "raw1_1_0")
-        for d, o in [(2, 1), (3, 0), (3, 1), (0, 0), (0, 1)]:
-            raws[d, o] = load_weight(d, o, 0, N)
+        turned = [psum.tile([P, 2, V], F32, name="turned%d" % u, tag="bank%d" % (4 + u)) for u in range(2)]
+
+        def turn(term, h, first=False, last=False):
+            for t in range(PACK):
+                nc.tensor.matmul(
+                    turned[t // 2][:, t % 2, h * P : (h + 1) * P],
+                    term[:, t, :],
+                    identity[:],
+                    is_transpose=True,
+                    start=(first and t % 2 == 0),
+                    stop=(last and t % 2 == 1),
+                )
+
+        banks1 = relation_banks("one", 0)
+        banks2 = relation_banks("two", 2)
+        relation_pass(1, 0, banks1, round_relation(1, 0, 256))
         for u in range(2):
             entries = slice(u * (S // 2), (u + 1) * (S // 2))
             list_cols = slice(u * (LIST_COLS // 2), (u + 1) * (LIST_COLS // 2))
-            nc.vector.tensor_copy(picked_words[1][:, entries], table1[:].indirect(offsets[:, list_cols]))
-        multiply_relation(1, 1, banks1, codes[:], scales[:])
+            nc.vector.tensor_copy(picked_words[1][:, entries], tables[1][:].indirect(offsets[:, list_cols]))
+        codes11 = relation_pass(1, 1, banks1, round_relation(1, 1, 320))
 
-        grouped = round_relation(raws[2, 0], 192, "2_0")
-        sums1 = [tile([P, PACK, P], F32, "sums1_%d" % h) for h in range(HALVES)]
-        nc.scalar.activation(sums1[0][:], dealt(banks1[0]), ACT.Copy, scale=edges[0][:, 0, :])
-        nc.vector.tensor_scalar_mul(sums1[1][:], dealt(banks1[1]), edges[0][:, 1, :])
-        relation_pass(2, 0, banks2, grouped)
-        relation_pass(2, 1, banks2, round_relation(raws[2, 1], 256, "2_1"))
-
-        grouped = round_relation(raws[3, 0], 128, "3_0")
-        sums2 = [tile([P, PACK, P], F32, "sums2_%d" % h) for h in range(HALVES)]
+        grouped = round_relation(2, 0, 384)
+        terms1 = spent_columns(raws[2, 0])
         for h in range(HALVES):
-            gated_sum(sums2[h][:], banks2[h], edges[1][:, h, :], sums1[h][:])
-        turned = [psum.tile([P, 2, V], F32, name="turned%d" % u, tag="rel%d" % (2 + u)) for u in range(2)]
+            gate_on_scalar(1, banks1, terms1, h)
+        codes20 = relation_pass(2, 0, banks2, grouped)
+        turn(terms1[1], 1, first=True)
+        codes21 = relation_pass(2, 1, banks2, round_relation(2, 1, 320))
 
-        def turn(terms, first):
-            for u in range(2):
-                for h in range(HALVES):
-                    for e in range(2):
-                        nc.tensor.matmul(
-                            turned[u][:, e, h * P : (h + 1) * P],
-                            terms[h][:, 2 * u + e, :],
-                            identity[:],
-                            is_transpose=True,
-                            start=(first and h == 0 and e == 0),
-                            stop=(not first and h == HALVES - 1 and e == 1),
-                        )
+        grouped = round_relation(3, 0, 288)
+        sum2 = raws[3, 0][:, :, 0:P]
+        nc.vector.scalar_tensor_tensor(sum2, dealt(banks2[0]), edges[1][:, 0, :], terms1[0], ALU.mult, ALU.add)
+        terms2 = spent_columns(raws[3, 0])[::-1]
+        gate_on_scalar(2, banks2, terms2, 1)
+        turn(sum2, 0)
+        turn(terms2[1], 1)
+        banks3 = relation_banks("three", 0)
+        codes30 = relation_pass(3, 0, banks3, grouped)
+        grouped31 = round_relation(3, 1, 320)
+        codes31 = relation_pass(3, 1, banks3, grouped31)
 
-        turn(sums2, True)
-        banks3 = relation_banks("three", 0, N)
-        relation_pass(3, 0, banks3, grouped)
-        relation_pass(3, 1, banks3, round_relation(raws[3, 1], 192, "3_1"))
-
-        def round_self(copy, o, pair, u, m0, m1):
+        def round_self(o, split):
             by_tile = raws[0, o][:].rearrange("p j (m t) -> p m j t", t=PACK)
-            copy(pair[:, :, m0:m1, :].rearrange("p t m j -> p m j t"), by_tile[:, m0:m1, :, 2 * u : 2 * u + 2])
-
-        pairs = [tile([P, 2, P, PACK], BF16, "self_grouped0_%d" % u) for u in range(2)]
-        round_self(nc.vector.tensor_copy, 0, pairs[0], 0, 0, P)
-        round_self(nc.scalar.copy, 0, pairs[1], 1, 0, P)
-
-        terms3 = [tile([P, PACK, P], F32, "terms3_%d" % h) for h in range(HALVES)]
-        for h in range(HALVES):
-            nc.scalar.activation(terms3[h][:], dealt(banks3[h]), ACT.Copy, scale=edges[2][:, h, :])
+            grouped = tile([P, PACK, P, PACK], BF16, "self_grouped%d" % o)
+            for u in range(2):
+                pair = slice(2 * u, 2 * u + 2)
+                for copy, m0, m1 in ((nc.vector.tensor_copy, 0, split), (nc.scalar.copy, split, P))[: 1 + (split < P)]:
+                    copy(grouped[:, pair, m0:m1, :].rearrange("p t m j -> p m j t"), by_tile[:, m0:m1, :, pair])
+            return grouped
 
         self_codes = [tile([P, PACK, P], U32, "self_codes%d" % o) for o in range(PASSES)]
         self_scales = [tile([P, PACK, P], U8, "self_scales%d" % o) for o in range(PASSES)]
-        self_banks = [psum.tile([P, V], F32, name="self_bank%d" % t, tag="self%d" % t) for t in range(PACK)]
+        self_banks = [psum.tile([P, V], F32, name="self_bank%d" % t, tag="bank%d" % (6, 7, 2, 3)[t]) for t in range(PACK)]
 
-        def multiply_self(o, t):
-            nc.tensor.matmul_mx(
-                out=self_banks[t][:],
-                lhsT=self_codes[o][:, t, :].bitcast(FP8X4),
-                lhsT_scale=self_scales[o][:, t, :],
-                rhs=picked_words[o][:, 0:V].bitcast(FP8X4),
-                rhs_scale=picked_scales[4 * o :, 0:V],
-                start=(o == 0),
-                stop=(o == PASSES - 1),
-            )
-
-        for u in (1, 0):
+        def self_pass(o, grouped, tiles):
             nc.vector.quantize_mx(
-                out=self_codes[0][:, 2 * u : 2 * u + 2, :].rearrange("p t m -> p (t m)").bitcast(FP8X4),
-                scales=self_scales[0][:, 2 * u : 2 * u + 2, :].rearrange("p t m -> p (t m)"),
-                in_=pairs[u][:].rearrange("p t m j -> p (t m j)"),
+                out=self_codes[o][:, tiles, :].rearrange("p t m -> p (t m)").bitcast(FP8X4),
+                scales=self_scales[o][:, tiles, :].rearrange("p t m -> p (t m)"),
+                in_=grouped[:, tiles].rearrange("p t m j -> p (t m j)"),
             )
-            for t in (2 * u, 2 * u + 1):
-                multiply_self(0, t)
+            for t in range(tiles.start, tiles.stop):
+                nc.tensor.matmul_mx(
+                    out=self_banks[t][:],
+                    lhsT=self_codes[o][:, t, :].bitcast(FP8X4),
+                    lhsT_scale=self_scales[o][:, t, :],
+                    rhs=picked_words[o][:, 0:V].bitcast(FP8X4),
+                    rhs_scale=picked_scales[4 * o :, 0:V],
+                    start=(o == 0),
+                    stop=(o == PASSES - 1),
+                )
 
-        turn(terms3, False)
-        pairs = [tile([P, 2, P, PACK], BF16, "self_grouped1_%d" % u) for u in range(2)]
-        round_self(nc.vector.tensor_copy, 1, pairs[0], 0, 0, P)
-        round_self(nc.scalar.copy, 1, pairs[1], 1, P // 2, P)
-        round_self(nc.vector.tensor_copy, 1, pairs[1], 1, 0, P // 2)
+        grouped = round_self(0, P)
+        terms3 = [tile([P, PACK, P], F32, "terms3_%d" % h)[:] for h in range(HALVES)]
+        for h in range(HALVES):
+            gate_on_scalar(3, banks3, terms3, h)
+            turn(terms3[h], h, last=(h == 1))
+        for u in range(2):
+            self_pass(0, grouped, slice(2 * u, 2 * u + 2))
+
+        grouped = round_self(1, 80)
         for t in range(PACK):
-            nc.vector.quantize_mx(
-                out=self_codes[1][:, t, :].bitcast(FP8X4),
-                scales=self_scales[1][:, t, :],
-                in_=pairs[t // 2][:, t % 2].rearrange("p m j -> p (m j)"),
-            )
-            multiply_self(1, t)
+            self_pass(1, grouped, slice(t, t + 1))
 
-        neighbours = tile([P, PACK, V], F32, "neighbours")
+        neighbours = raws[0, 1][:, :, :V]
         for t in range(PACK):
             nc.scalar.copy(neighbours[:, t, :], turned[t // 2][:, t % 2, :])
 
@@ -253,10 +227,12 @@ def tile_picked_zrgcn_relu_po_kernel(
             nc.vector.tensor_tensor(total[:, t, cols], self_banks[t][:, cols], neighbours[:, t, cols], ALU.add)
 
         out_rows = out_0.rearrange("(p t) v -> p t v", t=PACK)
-        for u in range(2):
-            result = tile([P, 2, V], F32, "result%d" % u)
-            nc.scalar.activation(result[:], total[:, 2 * u : 2 * u + 2, :], ACT.Relu)
-            nc.sync.dma_start(out_rows[:, 2 * u : 2 * u + 2, :], result[:])
+        result = tile([P, PACK, V], F32, "result")
+        for t in range(PACK):
+            nc.scalar.activation(result[:, t, :], total[:, t, :], ACT.Relu)
+            if t > 0:
+                rows = slice(0 if t == 1 else t, t + 1)
+                nc.sync.dma_start(out_rows[:, rows, :], result[:, rows, :])
 
         rounded = [tile([P, P, PACK], BF16, "rounded%d" % h) for h in range(HALVES)]
         for h in range(HALVES):
@@ -275,7 +251,7 @@ def tile_picked_zrgcn_relu_po_kernel(
                 scales=out_scales[:, cols],
                 in_=rounded[h][:].rearrange("p c t -> p (c t)"),
             )
-            nc.sync.dma_start(words_out[:, cols], out_codes[:, cols].bitcast(I32))
+        nc.sync.dma_start(words_out, out_codes[:].bitcast(I32))
         for q in range(QUADS):
             queue = nc.sync if q < 2 else nc.scalar
             queue.dma_start(out_2[0, 4 * q : 4 * q + 4, :].bitcast(I32), out_scales[32 * q : 32 * q + 4, :].bitcast(I32))

@@ -116,7 +116,7 @@ def tile_picked_zrgcn_relu_po_kernel(
                     start=(o == 0),
                     stop=(o == PASSES - 1),
                 )
-            return codes
+            return codes, scales
 
         def relation_banks(label, first):
             return [psum.tile([P, N], F32, name="%s%d" % (label, h), tag="bank%d" % (first + h)) for h in range(HALVES)]
@@ -168,9 +168,23 @@ def tile_picked_zrgcn_relu_po_kernel(
         turn(sum2, 0)
         turn(terms2[1], 1)
         banks3 = relation_banks("three", 0)
-        codes30 = relation_pass(3, 0, banks3, grouped)
+
+        def warm_up(quantised, width, label):
+            codes, scales = quantised
+            unread = psum.tile([P, width], F32, name=label, tag="bank7")
+            nc.tensor.matmul_mx(
+                out=unread[:],
+                lhsT=codes[:, 0:P].bitcast(FP8X4),
+                lhsT_scale=scales[:, 0:P],
+                rhs=codes[:, 0:width].bitcast(FP8X4),
+                rhs_scale=scales[:, 0:width],
+                start=True,
+                stop=True,
+            )
+
+        warm_up(relation_pass(3, 0, banks3, grouped), 256, "unread0")
         grouped31 = round_relation(3, 1, 320)
-        codes31 = relation_pass(3, 1, banks3, grouped31)
+        warm_up(relation_pass(3, 1, banks3, grouped31), 512, "unread1")
 
         def round_self(o, split):
             by_tile = raws[0, o][:].rearrange("p j (m t) -> p m j t", t=PACK)

@@ -189,10 +189,10 @@ def tile_picked_zrgcn_relu_po_kernel(
         def round_self(o, split):
             by_tile = raws[0, o][:].rearrange("p j (m t) -> p m j t", t=PACK)
             grouped = tile([P, PACK, P, PACK], BF16, "self_grouped%d" % o)
-            for u in range(2):
+            nc.vector.tensor_copy(grouped[:, :, :split, :].rearrange("p t m j -> p m j t"), by_tile[:, :split])
+            for u in range(2 * (split < P)):
                 pair = slice(2 * u, 2 * u + 2)
-                for copy, m0, m1 in ((nc.vector.tensor_copy, 0, split), (nc.scalar.copy, split, P))[: 1 + (split < P)]:
-                    copy(grouped[:, pair, m0:m1, :].rearrange("p t m j -> p m j t"), by_tile[:, m0:m1, :, pair])
+                nc.scalar.copy(grouped[:, pair, split:, :].rearrange("p t m j -> p m j t"), by_tile[:, split:, :, pair])
             return grouped
 
         self_codes = [tile([P, PACK, P], U32, "self_codes%d" % o) for o in range(PASSES)]
@@ -224,7 +224,7 @@ def tile_picked_zrgcn_relu_po_kernel(
         for u in range(2):
             self_pass(0, grouped, slice(2 * u, 2 * u + 2))
 
-        grouped = round_self(1, 80)
+        grouped = round_self(1, 68)
         for t in range(PACK):
             self_pass(1, grouped, slice(t, t + 1))
 

@@ -183,17 +183,34 @@ def tile_picked_zrgcn_relu_po_kernel(
             )
 
         warm_up(relation_pass(3, 0, banks3, grouped), 256, "unread0")
-        grouped31 = round_relation(3, 1, 320)
-        warm_up(relation_pass(3, 1, banks3, grouped31), 512, "unread1")
-
-        def round_self(o, split):
-            by_tile = raws[0, o][:].rearrange("p j (m t) -> p m j t", t=PACK)
-            grouped = tile([P, PACK, P, PACK], BF16, "self_grouped%d" % o)
-            nc.vector.tensor_copy(grouped[:, :, :split, :].rearrange("p t m j -> p m j t"), by_tile[:, :split])
-            for u in range(2 * (split < P)):
-                pair = slice(2 * u, 2 * u + 2)
-                nc.scalar.copy(grouped[:, pair, split:, :].rearrange("p t m j -> p m j t"), by_tile[:, split:, :, pair])
-            return grouped
+        raw = raws[3, 1]
+        grouped = tile([P, N, PACK], BF16, "grouped3_1")
+        for copy, c0, c1 in ((nc.vector.tensor_copy, 0, 256), (nc.vector.tensor_copy, 256, 320), (nc.scalar.copy, 320, N)):
+            copy(
+                grouped[:, c0:c1, :].rearrange("p (c i) j -> p c j i", i=4),
+                raw[:, :, c0:c1].rearrange("p j (c i) -> p c j i", i=4),
+            )
+        codes31 = tile([P, N], U32, "codes3_1")
+        scales31 = tile([P, N], U8, "scales3_1")
+        for u in range(2):
+            half = slice(u * N // 2, (u + 1) * N // 2)
+            nc.vector.quantize_mx(
+                out=codes31[:, half].bitcast(FP8X4),
+                scales=scales31[:, half],
+                in_=grouped[:, half, :].rearrange("p c j -> p (c j)"),
+            )
+            for h in range(HALVES):
+                cols = slice(3 * V + h * P, 3 * V + (h + 1) * P)
+                nc.tensor.matmul_mx(
+                    out=banks3[h][:, half],
+                    lhsT=picked_words[1][:, cols].bitcast(FP8X4),
+                    lhsT_scale=picked_scales[4:, cols],
+                    rhs=codes31[:, half].bitcast(FP8X4),
+                    rhs_scale=scales31[:, half],
+                    start=False,
+                    stop=(u == 1),
+                )
+        warm_up((codes31, scales31), 512, "unread1")
 
         self_codes = [tile([P, PACK, P], U32, "self_codes%d" % o) for o in range(PASSES)]
         self_scales = [tile([P, PACK, P], U8, "self_scales%d" % o) for o in range(PASSES)]
@@ -216,7 +233,10 @@ def tile_picked_zrgcn_relu_po_kernel(
                     stop=(o == PASSES - 1),
                 )
 
-        grouped = round_self(0, P)
+        grouped = tile([P, PACK, P, PACK], BF16, "self_grouped0")
+        by_tile = raws[0, 0][:].rearrange("p j (m t) -> p m j t", t=PACK)
+        for tiles, m0, m1 in ((slice(0, 4), 0, 96), (slice(0, 2), 96, P), (slice(2, 4), 96, P)):
+            nc.vector.tensor_copy(grouped[:, tiles, m0:m1, :].rearrange("p t m j -> p m j t"), by_tile[:, m0:m1, :, tiles])
         terms3 = [tile([P, PACK, P], F32, "terms3_%d" % h)[:] for h in range(HALVES)]
         for h in range(HALVES):
             gate_on_scalar(3, banks3, terms3, h)
@@ -224,21 +244,36 @@ def tile_picked_zrgcn_relu_po_kernel(
         for u in range(2):
             self_pass(0, grouped, slice(2 * u, 2 * u + 2))
 
-        grouped = round_self(1, 68)
-        for t in range(PACK):
+        grouped = tile([P, PACK, P, PACK], BF16, "self_grouped1")
+        by_tile = raws[0, 1][:].rearrange("p j (m t) -> p m j t", t=PACK)
+
+        def round_last(copy, u, m0, m1):
+            pair = slice(2 * u, 2 * u + 2)
+            copy(grouped[:, pair, m0:m1, :].rearrange("p t m j -> p m j t"), by_tile[:, m0:m1, :, pair])
+
+        round_last(nc.vector.tensor_copy, 0, 0, 80)
+        round_last(nc.scalar.copy, 0, 80, P)
+        round_last(nc.scalar.copy, 1, 88, P)
+        round_last(nc.vector.tensor_copy, 1, 0, 40)
+        self_pass(1, grouped, slice(0, 1))
+        round_last(nc.vector.tensor_copy, 1, 40, 88)
+        for t in range(1, PACK):
             self_pass(1, grouped, slice(t, t + 1))
 
-        neighbours = raws[0, 1][:, :, :V]
+        def by_halves(ap):
+            return ap.rearrange("p (h v) -> p h v", h=HALVES)
+
+        neighbours = [raws[0, 1][:, 2 * (t % 2) : 2 * (t % 2) + 2, (t // 2) * P : (t // 2 + 1) * P] for t in range(PACK)]
         for t in range(PACK):
-            nc.scalar.copy(neighbours[:, t, :], turned[t // 2][:, t % 2, :])
+            nc.scalar.copy(neighbours[t], by_halves(turned[t // 2][:, t % 2, :]))
 
         total = tile([P, PACK, V], F32, "total")
         for t in range(PACK - 1):
-            nc.vector.tensor_tensor(total[:, t, :], self_banks[t][:], neighbours[:, t, :], ALU.add)
+            nc.vector.tensor_tensor(by_halves(total[:, t, :]), by_halves(self_banks[t][:]), neighbours[t], ALU.add)
         t = PACK - 1
         for h in range(HALVES):
             cols = slice(h * P, (h + 1) * P)
-            nc.vector.tensor_tensor(total[:, t, cols], self_banks[t][:, cols], neighbours[:, t, cols], ALU.add)
+            nc.vector.tensor_tensor(total[:, t, cols], self_banks[t][:, cols], neighbours[t][:, h, :], ALU.add)
 
         out_rows = out_0.rearrange("(p t) v -> p t v", t=PACK)
         result = tile([P, PACK, V], F32, "result")

@@ -216,6 +216,8 @@ def tile_picked_zrgcn_relu_po_kernel(
         self_scales = [tile([P, PACK, P], U8, "self_scales%d" % o) for o in range(PASSES)]
         self_banks = [psum.tile([P, V], F32, name="self_bank%d" % t, tag="bank%d" % (6, 7, 2, 3)[t]) for t in range(PACK)]
 
+        first_halves = [self_banks[0][:, :P], psum.tile([P, P], F32, name="self_bank0_1", tag="bank0")[:]]
+
         def self_pass(o, grouped, tiles):
             nc.vector.quantize_mx(
                 out=self_codes[o][:, tiles, :].rearrange("p t m -> p (t m)").bitcast(FP8X4),
@@ -223,15 +225,19 @@ def tile_picked_zrgcn_relu_po_kernel(
                 in_=grouped[:, tiles].rearrange("p t m j -> p (t m j)"),
             )
             for t in range(tiles.start, tiles.stop):
-                nc.tensor.matmul_mx(
-                    out=self_banks[t][:],
-                    lhsT=self_codes[o][:, t, :].bitcast(FP8X4),
-                    lhsT_scale=self_scales[o][:, t, :],
-                    rhs=picked_words[o][:, 0:V].bitcast(FP8X4),
-                    rhs_scale=picked_scales[4 * o :, 0:V],
-                    start=(o == 0),
-                    stop=(o == PASSES - 1),
-                )
+                pieces = [(self_banks[t][:], 0, V)]
+                if t == 0:
+                    pieces = [(first_halves[h], h * P, (h + 1) * P) for h in range(HALVES)]
+                for bank, v0, v1 in pieces:
+                    nc.tensor.matmul_mx(
+                        out=bank,
+                        lhsT=self_codes[o][:, t, :].bitcast(FP8X4),
+                        lhsT_scale=self_scales[o][:, t, :],
+                        rhs=picked_words[o][:, v0:v1].bitcast(FP8X4),
+                        rhs_scale=picked_scales[4 * o :, v0:v1],
+                        start=(o == 0),
+                        stop=(o == PASSES - 1),
+                    )
 
         grouped = tile([P, PACK, P, PACK], BF16, "self_grouped0")
         by_tile = raws[0, 0][:].rearrange("p j (m t) -> p m j t", t=PACK)
@@ -239,7 +245,9 @@ def tile_picked_zrgcn_relu_po_kernel(
             nc.vector.tensor_copy(grouped[:, tiles, m0:m1, :].rearrange("p t m j -> p m j t"), by_tile[:, m0:m1, :, tiles])
         terms3 = [tile([P, PACK, P], F32, "terms3_%d" % h)[:] for h in range(HALVES)]
         for h in range(HALVES):
-            gate_on_scalar(3, banks3, terms3, h)
+            for u in range(2):
+                pair = slice(2 * u, 2 * u + 2)
+                nc.scalar.activation(terms3[h][:, pair], dealt(banks3[h])[:, pair], ACT.Copy, scale=edges[2][:, h, :])
             turn(terms3[h], h, last=(h == 1))
         for u in range(2):
             self_pass(0, grouped, slice(2 * u, 2 * u + 2))
@@ -268,7 +276,10 @@ def tile_picked_zrgcn_relu_po_kernel(
             nc.scalar.copy(neighbours[t], by_halves(turned[t // 2][:, t % 2, :]))
 
         total = tile([P, PACK, V], F32, "total")
-        for t in range(PACK - 1):
+        for h in range(HALVES):
+            cols = slice(h * P, (h + 1) * P)
+            nc.vector.tensor_tensor(total[:, 0, cols], first_halves[h], neighbours[0][:, h, :], ALU.add)
+        for t in range(1, PACK - 1):
             nc.vector.tensor_tensor(by_halves(total[:, t, :]), by_halves(self_banks[t][:]), neighbours[t], ALU.add)
         t = PACK - 1
         for h in range(HALVES):

@@ -160,29 +160,18 @@ def tile_picked_zrgcn_relu_po_kernel(
         turn(terms1[1], 1, first=True)
         codes21 = relation_pass(2, 1, banks2, round_relation(2, 1, 320))
 
-        grouped = round_relation(3, 0, 288)
-        sum2 = raws[3, 0][:, :, 0:P]
-        nc.vector.scalar_tensor_tensor(sum2, dealt(banks2[0]), edges[1][:, 0, :], terms1[0], ALU.mult, ALU.add)
-        terms2 = spent_columns(raws[3, 0])[::-1]
-        gate_on_scalar(2, banks2, terms2, 1)
-        turn(sum2, 0)
-        turn(terms2[1], 1)
-        banks3 = relation_banks("three", 0)
-
-        def warm_up(quantised, width, label):
-            codes, scales = quantised
-            unread = psum.tile([P, width], F32, name=label, tag="bank7")
-            nc.tensor.matmul_mx(
-                out=unread[:],
-                lhsT=codes[:, 0:P].bitcast(FP8X4),
-                lhsT_scale=scales[:, 0:P],
-                rhs=codes[:, 0:width].bitcast(FP8X4),
-                rhs_scale=scales[:, 0:width],
-                start=True,
-                stop=True,
+        raw = raws[3, 0]
+        grouped = tile([P, N, PACK], BF16, "grouped3_0")
+        for copy, c0, c1 in ((nc.vector.tensor_copy, 0, P), (nc.vector.tensor_copy, P, 288), (nc.scalar.copy, 288, N)):
+            copy(
+                grouped[:, c0:c1, :].rearrange("p (c i) j -> p c j i", i=4),
+                raw[:, :, c0:c1].rearrange("p j (c i) -> p c j i", i=4),
             )
-
-        warm_up(relation_pass(3, 0, banks3, grouped), 256, "unread0")
+        sum2 = raw[:, :, 0:P]
+        nc.vector.scalar_tensor_tensor(sum2, dealt(banks2[0]), edges[1][:, 0, :], terms1[0], ALU.mult, ALU.add)
+        turn(sum2, 0)
+        banks3 = relation_banks("three", 0)
+        q30 = relation_pass(3, 0, banks3, grouped)
         raw = raws[3, 1]
         grouped = tile([P, N, PACK], BF16, "grouped3_1")
         for copy, c0, c1 in ((nc.vector.tensor_copy, 0, 256), (nc.vector.tensor_copy, 256, 320), (nc.scalar.copy, 320, N)):
@@ -210,7 +199,9 @@ def tile_picked_zrgcn_relu_po_kernel(
                     start=False,
                     stop=(u == 1),
                 )
-        warm_up((codes31, scales31), 512, "unread1")
+        spent = grouped[:, : N // 2, :].rearrange("p c j -> p (c j)").bitcast(F32).rearrange("p (t m) -> p t m", t=PACK)
+        gate_on_scalar(2, banks2, [None, spent], 1)
+        turn(spent, 1)
 
         self_codes = [tile([P, PACK, P], U32, "self_codes%d" % o) for o in range(PASSES)]
         self_scales = [tile([P, PACK, P], U8, "self_scales%d" % o) for o in range(PASSES)]

@@ -199,6 +199,17 @@ def tile_picked_zrgcn_relu_po_kernel(
                     start=False,
                     stop=(u == 1),
                 )
+        for width in (N, N // 2):
+            unread = psum.tile([P, width], F32, name="unread%d" % width, tag="bank7")
+            nc.tensor.matmul_mx(
+                out=unread[:],
+                lhsT=codes31[:, 0:P].bitcast(FP8X4),
+                lhsT_scale=scales31[:, 0:P],
+                rhs=codes31[:, 0:width].bitcast(FP8X4),
+                rhs_scale=scales31[:, 0:width],
+                start=True,
+                stop=True,
+            )
         spent = grouped[:, : N // 2, :].rearrange("p c j -> p (c j)").bitcast(F32).rearrange("p (t m) -> p t m", t=PACK)
         gate_on_scalar(2, banks2, [None, spent], 1)
         turn(spent, 1)

@@ -132,8 +132,8 @@ def tile_picked_zrgcn_relu_po_kernel(
 
         turned = [psum.tile([P, 2, V], F32, name="turned%d" % u, tag="bank%d" % (4 + u)) for u in range(2)]
 
-        def turn(term, h, first=False, last=False):
-            for t in range(PACK):
+        def turn(term, h, first=False, last=False, tiles=range(PACK)):
+            for t in tiles:
                 nc.tensor.matmul(
                     turned[t // 2][:, t % 2, h * P : (h + 1) * P],
                     term[:, t, :],
@@ -160,59 +160,71 @@ def tile_picked_zrgcn_relu_po_kernel(
         turn(terms1[1], 1, first=True)
         codes21 = relation_pass(2, 1, banks2, round_relation(2, 1, 320))
 
-        raw = raws[3, 0]
-        grouped = tile([P, N, PACK], BF16, "grouped3_0")
-        for copy, c0, c1 in ((nc.vector.tensor_copy, 0, P), (nc.vector.tensor_copy, P, 288), (nc.scalar.copy, 288, N)):
-            copy(
-                grouped[:, c0:c1, :].rearrange("p (c i) j -> p c j i", i=4),
-                raw[:, :, c0:c1].rearrange("p j (c i) -> p c j i", i=4),
-            )
-        sum2 = raw[:, :, 0:P]
-        nc.vector.scalar_tensor_tensor(sum2, dealt(banks2[0]), edges[1][:, 0, :], terms1[0], ALU.mult, ALU.add)
-        turn(sum2, 0)
-        banks3 = relation_banks("three", 0)
-        q30 = relation_pass(3, 0, banks3, grouped)
-        raw = raws[3, 1]
-        grouped = tile([P, N, PACK], BF16, "grouped3_1")
-        for copy, c0, c1 in ((nc.vector.tensor_copy, 0, 256), (nc.vector.tensor_copy, 256, 320), (nc.scalar.copy, 320, N)):
-            copy(
-                grouped[:, c0:c1, :].rearrange("p (c i) j -> p c j i", i=4),
-                raw[:, :, c0:c1].rearrange("p j (c i) -> p c j i", i=4),
-            )
-        codes31 = tile([P, N], U32, "codes3_1")
-        scales31 = tile([P, N], U8, "scales3_1")
-        for u in range(2):
-            half = slice(u * N // 2, (u + 1) * N // 2)
-            nc.vector.quantize_mx(
-                out=codes31[:, half].bitcast(FP8X4),
-                scales=scales31[:, half],
-                in_=grouped[:, half, :].rearrange("p c j -> p (c j)"),
-            )
+        def round_dealt(copy, grouped, raw, u, m0, m1):
+            pair = slice(2 * u, 2 * u + 2)
+            by_tile = raw[:].rearrange("p j (m t) -> p m j t", t=PACK)
+            copy(grouped[:, pair, m0:m1, :].rearrange("p t m j -> p m j t"), by_tile[:, m0:m1, :, pair])
+
+        second_pair = psum.tile([P, HALVES, V], F32, name="three1", tag="bank1")
+        banks3 = [
+            [psum.tile([P, V], F32, name="three0_%d" % h, tag="bank%d" % (0, 6)[h])[:] for h in range(HALVES)],
+            [second_pair[:, h, :] for h in range(HALVES)],
+        ]
+
+        def last_relation(o, u, grouped, codes, scales):
+            pair = slice(2 * u, 2 * u + 2)
+            words = codes[:, pair].rearrange("p t m -> p (t m)").bitcast(FP8X4)
+            plane = scales[:, pair].rearrange("p t m -> p (t m)")
+            nc.vector.quantize_mx(out=words, scales=plane, in_=grouped[:, pair].rearrange("p t m j -> p (t m j)"))
             for h in range(HALVES):
                 cols = slice(3 * V + h * P, 3 * V + (h + 1) * P)
                 nc.tensor.matmul_mx(
-                    out=banks3[h][:, half],
-                    lhsT=picked_words[1][:, cols].bitcast(FP8X4),
-                    lhsT_scale=picked_scales[4:, cols],
-                    rhs=codes31[:, half].bitcast(FP8X4),
-                    rhs_scale=scales31[:, half],
-                    start=False,
-                    stop=(u == 1),
+                    out=banks3[u][h],
+                    lhsT=picked_words[o][:, cols].bitcast(FP8X4),
+                    lhsT_scale=picked_scales[4 * o :, cols],
+                    rhs=words,
+                    rhs_scale=plane,
+                    start=(o == 0 and (u == 0 or h == 0)),
+                    stop=(o == PASSES - 1 and (u == 0 or h == 1)),
                 )
-        for width in (N, N // 2):
-            unread = psum.tile([P, width], F32, name="unread%d" % width, tag="bank7")
-            nc.tensor.matmul_mx(
-                out=unread[:],
-                lhsT=codes31[:, 0:P].bitcast(FP8X4),
-                lhsT_scale=scales31[:, 0:P],
-                rhs=codes31[:, 0:width].bitcast(FP8X4),
-                rhs_scale=scales31[:, 0:width],
-                start=True,
-                stop=True,
-            )
-        spent = grouped[:, : N // 2, :].rearrange("p c j -> p (c j)").bitcast(F32).rearrange("p (t m) -> p t m", t=PACK)
+
+        raw = raws[3, 0]
+        grouped = tile([P, PACK, P, PACK], BF16, "grouped3_0")
+        by_tile = raw[:].rearrange("p j (m t) -> p m j t", t=PACK)
+        for copy, m0, m1 in ((nc.vector.tensor_copy, 0, 32), (nc.vector.tensor_copy, 32, 72)):
+            copy(grouped[:, :, m0:m1, :].rearrange("p t m j -> p m j t"), by_tile[:, m0:m1])
+        for u in range(2):
+            round_dealt(nc.scalar.copy, grouped, raw, u, 72, P)
+        sum2 = raw[:, :, 0:P]
+        nc.vector.scalar_tensor_tensor(sum2, dealt(banks2[0]), edges[1][:, 0, :], terms1[0], ALU.mult, ALU.add)
+        turn(sum2, 0)
+        spent = raw[:, :, N - P : N]
         gate_on_scalar(2, banks2, [None, spent], 1)
         turn(spent, 1)
+        codes30 = tile([P, PACK, P], U32, "codes3_0")
+        scales30 = tile([P, PACK, P], U8, "scales3_0")
+        for u in range(2):
+            last_relation(0, u, grouped, codes30, scales30)
+        raw = raws[3, 1]
+        grouped = tile([P, PACK, P, PACK], BF16, "grouped3_1")
+        for u in range(2):
+            round_dealt(nc.vector.tensor_copy, grouped, raw, u, 0, 80)
+            round_dealt(nc.scalar.copy, grouped, raw, u, 80, P)
+        codes = tile([P, PACK, P], U32, "codes3_1")
+        scales = tile([P, PACK, P], U8, "scales3_1")
+        for u in range(2):
+            last_relation(1, u, grouped, codes, scales)
+
+        terms3 = [tile([P, PACK, P], F32, "terms3_%d" % h)[:] for h in range(HALVES)]
+        for u in range(2):
+            pair = slice(2 * u, 2 * u + 2)
+            for h in range(HALVES):
+                sums = banks3[u][h].rearrange("v (t m) -> v t m", t=2)
+                if u == 0 and h == 1:
+                    nc.vector.tensor_scalar_mul(terms3[h][:, pair], sums, edges[2][:, h, :])
+                else:
+                    nc.scalar.activation(terms3[h][:, pair], sums, ACT.Copy, scale=edges[2][:, h, :])
+                turn(terms3[h], h, last=(h == 1), tiles=range(2 * u, 2 * u + 2))
 
         self_codes = [tile([P, PACK, P], U32, "self_codes%d" % o) for o in range(PASSES)]
         self_scales = [tile([P, PACK, P], U8, "self_scales%d" % o) for o in range(PASSES)]
@@ -245,12 +257,6 @@ def tile_picked_zrgcn_relu_po_kernel(
         by_tile = raws[0, 0][:].rearrange("p j (m t) -> p m j t", t=PACK)
         for tiles, m0, m1 in ((slice(0, 4), 0, 96), (slice(0, 2), 96, P), (slice(2, 4), 96, P)):
             nc.vector.tensor_copy(grouped[:, tiles, m0:m1, :].rearrange("p t m j -> p m j t"), by_tile[:, m0:m1, :, tiles])
-        terms3 = [tile([P, PACK, P], F32, "terms3_%d" % h)[:] for h in range(HALVES)]
-        for h in range(HALVES):
-            for u in range(2):
-                pair = slice(2 * u, 2 * u + 2)
-                nc.scalar.activation(terms3[h][:, pair], dealt(banks3[h])[:, pair], ACT.Copy, scale=edges[2][:, h, :])
-            turn(terms3[h], h, last=(h == 1))
         for u in range(2):
             self_pass(0, grouped, slice(2 * u, 2 * u + 2))
 
@@ -273,9 +279,10 @@ def tile_picked_zrgcn_relu_po_kernel(
         def by_halves(ap):
             return ap.rearrange("p (h v) -> p h v", h=HALVES)
 
-        neighbours = [raws[0, 1][:, 2 * (t % 2) : 2 * (t % 2) + 2, (t // 2) * P : (t // 2 + 1) * P] for t in range(PACK)]
-        for t in range(PACK):
-            nc.scalar.copy(neighbours[t], by_halves(turned[t // 2][:, t % 2, :]))
+        summed = tile([P, PACK, V], F32, "summed")
+        for u in range(2):
+            nc.scalar.copy(summed[:, 2 * u : 2 * u + 2, :], turned[u][:])
+        neighbours = [by_halves(summed[:, t, :]) for t in range(PACK)]
 
         total = tile([P, PACK, V], F32, "total")
         for h in range(HALVES):

@@ -226,6 +226,20 @@ def tile_picked_zrgcn_relu_po_kernel(
                     nc.scalar.activation(terms3[h][:, pair], sums, ACT.Copy, scale=edges[2][:, h, :])
                 turn(terms3[h], h, last=(h == 1), tiles=range(2 * u, 2 * u + 2))
 
+        def warm_up(name, words, plane, width):
+            unread = psum.tile([P, width], F32, name=name, tag="bank1")
+            nc.tensor.matmul_mx(
+                out=unread[:],
+                lhsT=words[:, 0:P].bitcast(FP8X4),
+                lhsT_scale=plane[:, 0:P],
+                rhs=words[:, 0:width].bitcast(FP8X4),
+                rhs_scale=plane[:, 0:width],
+                start=True,
+                stop=True,
+            )
+
+        warm_up("unread0", codes[:].rearrange("p t m -> p (t m)"), scales[:].rearrange("p t m -> p (t m)"), V)
+
         self_codes = [tile([P, PACK, P], U32, "self_codes%d" % o) for o in range(PASSES)]
         self_scales = [tile([P, PACK, P], U8, "self_scales%d" % o) for o in range(PASSES)]
         self_banks = [psum.tile([P, V], F32, name="self_bank%d" % t, tag="bank%d" % (6, 7, 2, 3)[t]) for t in range(PACK)]
@@ -259,6 +273,7 @@ def tile_picked_zrgcn_relu_po_kernel(
             nc.vector.tensor_copy(grouped[:, tiles, m0:m1, :].rearrange("p t m j -> p m j t"), by_tile[:, m0:m1, :, tiles])
         for u in range(2):
             self_pass(0, grouped, slice(2 * u, 2 * u + 2))
+        warm_up("unread1", self_codes[0][:].rearrange("p t m -> p (t m)"), self_scales[0][:].rearrange("p t m -> p (t m)"), N)
 
         grouped = tile([P, PACK, P, PACK], BF16, "self_grouped1")
         by_tile = raws[0, 1][:].rearrange("p j (m t) -> p m j t", t=PACK)

@@ -165,6 +165,18 @@ def tile_picked_zrgcn_relu_po_kernel(
             by_tile = raw[:].rearrange("p j (m t) -> p m j t", t=PACK)
             copy(grouped[:, pair, m0:m1, :].rearrange("p t m j -> p m j t"), by_tile[:, m0:m1, :, pair])
 
+        def warm_up(name, words, plane, width, bank):
+            unread = psum.tile([P, width], F32, name=name, tag=bank)
+            nc.tensor.matmul_mx(
+                out=unread[:],
+                lhsT=words[:, 0:P].bitcast(FP8X4),
+                lhsT_scale=plane[:, 0:P],
+                rhs=words[:, 0:width].bitcast(FP8X4),
+                rhs_scale=plane[:, 0:width],
+                start=True,
+                stop=True,
+            )
+
         second_pair = psum.tile([P, HALVES, V], F32, name="three1", tag="bank1")
         banks3 = [
             [psum.tile([P, V], F32, name="three0_%d" % h, tag="bank%d" % (0, 6)[h])[:] for h in range(HALVES)],
@@ -205,6 +217,7 @@ def tile_picked_zrgcn_relu_po_kernel(
         scales30 = tile([P, PACK, P], U8, "scales3_0")
         for u in range(2):
             last_relation(0, u, grouped, codes30, scales30)
+        warm_up("unread2", codes30[:, 2:].rearrange("p t m -> p (t m)"), scales30[:, 2:].rearrange("p t m -> p (t m)"), V, "bank7")
         raw = raws[3, 1]
         grouped = tile([P, PACK, P, PACK], BF16, "grouped3_1")
         for u in range(2):
@@ -226,19 +239,7 @@ def tile_picked_zrgcn_relu_po_kernel(
                     nc.scalar.activation(terms3[h][:, pair], sums, ACT.Copy, scale=edges[2][:, h, :])
                 turn(terms3[h], h, last=(h == 1), tiles=range(2 * u, 2 * u + 2))
 
-        def warm_up(name, words, plane, width):
-            unread = psum.tile([P, width], F32, name=name, tag="bank1")
-            nc.tensor.matmul_mx(
-                out=unread[:],
-                lhsT=words[:, 0:P].bitcast(FP8X4),
-                lhsT_scale=plane[:, 0:P],
-                rhs=words[:, 0:width].bitcast(FP8X4),
-                rhs_scale=plane[:, 0:width],
-                start=True,
-                stop=True,
-            )
-
-        warm_up("unread0", codes[:].rearrange("p t m -> p (t m)"), scales[:].rearrange("p t m -> p (t m)"), V)
+        warm_up("unread0", codes[:].rearrange("p t m -> p (t m)"), scales[:].rearrange("p t m -> p (t m)"), V, "bank1")
 
         self_codes = [tile([P, PACK, P], U32, "self_codes%d" % o) for o in range(PASSES)]
         self_scales = [tile([P, PACK, P], U8, "self_scales%d" % o) for o in range(PASSES)]
@@ -273,7 +274,7 @@ def tile_picked_zrgcn_relu_po_kernel(
             nc.vector.tensor_copy(grouped[:, tiles, m0:m1, :].rearrange("p t m j -> p m j t"), by_tile[:, m0:m1, :, tiles])
         for u in range(2):
             self_pass(0, grouped, slice(2 * u, 2 * u + 2))
-        warm_up("unread1", self_codes[0][:].rearrange("p t m -> p (t m)"), self_scales[0][:].rearrange("p t m -> p (t m)"), N)
+        warm_up("unread1", self_codes[0][:, 2:].rearrange("p t m -> p (t m)"), self_scales[0][:, 2:].rearrange("p t m -> p (t m)"), V, "bank1")
 
         grouped = tile([P, PACK, P, PACK], BF16, "self_grouped1")
         by_tile = raws[0, 1][:].rearrange("p j (m t) -> p m j t", t=PACK)
@@ -312,19 +313,24 @@ def tile_picked_zrgcn_relu_po_kernel(
 
         out_rows = out_0.rearrange("(p t) v -> p t v", t=PACK)
         result = tile([P, PACK, V], F32, "result")
+        rounded = tile([P, V, PACK], BF16, "rounded")
+
+        def round_result(c0, c1):
+            return (
+                rounded[:, c0:c1, :].rearrange("p (c i) t -> p c t i", i=4),
+                total[:, :, c0:c1].rearrange("p t (c i) -> p c t i", i=4),
+            )
+
         for t in range(PACK):
+            if t == PACK - 1:
+                nc.scalar.activation(*round_result(160, V), ACT.Relu)
             nc.scalar.activation(result[:, t, :], total[:, t, :], ACT.Relu)
             if t > 0:
                 rows = slice(0 if t == 1 else t, t + 1)
                 nc.sync.dma_start(out_rows[:, rows, :], result[:, rows, :])
 
-        rounded = [tile([P, P, PACK], BF16, "rounded%d" % h) for h in range(HALVES)]
-        for h in range(HALVES):
-            nc.vector.tensor_scalar_max(
-                rounded[h][:].rearrange("p (c i) t -> p c t i", i=4),
-                total[:, :, h * P : (h + 1) * P].rearrange("p t (c i) -> p c t i", i=4),
-                0.0,
-            )
+        for c0, c1 in ((0, P), (P, 160)):
+            nc.vector.tensor_scalar_max(*round_result(c0, c1), 0.0)
         out_codes = tile([P, V], U32, "out_codes")
         out_scales = tile([P, V], U8, "out_scales")
         words_out = out_1[0].rearrange("p c r -> p (c r)").bitcast(I32)
@@ -333,7 +339,7 @@ def tile_picked_zrgcn_relu_po_kernel(
             nc.vector.quantize_mx(
                 out=out_codes[:, cols].bitcast(FP8X4),
                 scales=out_scales[:, cols],
-                in_=rounded[h][:].rearrange("p c t -> p (c t)"),
+                in_=rounded[:, cols, :].rearrange("p c t -> p (c t)"),
             )
         nc.sync.dma_start(words_out, out_codes[:].bitcast(I32))
         for q in range(QUADS):

@@ -233,10 +233,7 @@ def tile_picked_zrgcn_relu_po_kernel(
             pair = slice(2 * u, 2 * u + 2)
             for h in range(HALVES):
                 sums = banks3[u][h].rearrange("v (t m) -> v t m", t=2)
-                if u == 0 and h == 1:
-                    nc.vector.tensor_scalar_mul(terms3[h][:, pair], sums, edges[2][:, h, :])
-                else:
-                    nc.scalar.activation(terms3[h][:, pair], sums, ACT.Copy, scale=edges[2][:, h, :])
+                nc.scalar.activation(terms3[h][:, pair], sums, ACT.Copy, scale=edges[2][:, h, :])
                 turn(terms3[h], h, last=(h == 1), tiles=range(2 * u, 2 * u + 2))
 
         warm_up("unread0", codes[:].rearrange("p t m -> p (t m)"), scales[:].rearrange("p t m -> p (t m)"), V, "bank1")

@@ -209,6 +209,7 @@ def tile_picked_zrgcn_relu_po_kernel(
             round_dealt(nc.scalar.copy, grouped, raw, u, 72, P)
         sum2 = raw[:, :, 0:P]
         nc.vector.scalar_tensor_tensor(sum2, dealt(banks2[0]), edges[1][:, 0, :], terms1[0], ALU.mult, ALU.add)
+        warm_up("unread2", codes21[0][:], codes21[1][:], N, "bank2")
         turn(sum2, 0)
         spent = raw[:, :, N - P : N]
         gate_on_scalar(2, banks2, [None, spent], 1)
@@ -217,7 +218,6 @@ def tile_picked_zrgcn_relu_po_kernel(
         scales30 = tile([P, PACK, P], U8, "scales3_0")
         for u in range(2):
             last_relation(0, u, grouped, codes30, scales30)
-        warm_up("unread2", codes30[:, 2:].rearrange("p t m -> p (t m)"), scales30[:, 2:].rearrange("p t m -> p (t m)"), V, "bank7")
         raw = raws[3, 1]
         grouped = tile([P, PACK, P, PACK], BF16, "grouped3_1")
         for u in range(2):
@@ -271,7 +271,6 @@ def tile_picked_zrgcn_relu_po_kernel(
             nc.vector.tensor_copy(grouped[:, tiles, m0:m1, :].rearrange("p t m j -> p m j t"), by_tile[:, m0:m1, :, tiles])
         for u in range(2):
             self_pass(0, grouped, slice(2 * u, 2 * u + 2))
-        warm_up("unread1", self_codes[0][:, 2:].rearrange("p t m -> p (t m)"), self_scales[0][:, 2:].rearrange("p t m -> p (t m)"), V, "bank1")
 
         grouped = tile([P, PACK, P, PACK], BF16, "self_grouped1")
         by_tile = raws[0, 1][:].rearrange("p j (m t) -> p m j t", t=PACK)
@@ -286,8 +285,8 @@ def tile_picked_zrgcn_relu_po_kernel(
         round_last(nc.vector.tensor_copy, 1, 0, 40)
         self_pass(1, grouped, slice(0, 1))
         round_last(nc.vector.tensor_copy, 1, 40, 88)
-        for t in range(1, PACK):
-            self_pass(1, grouped, slice(t, t + 1))
+        for tiles in (slice(1, 2), slice(2, 4)):
+            self_pass(1, grouped, tiles)
 
         def by_halves(ap):
             return ap.rearrange("p (h v) -> p h v", h=HALVES)
@@ -319,14 +318,13 @@ def tile_picked_zrgcn_relu_po_kernel(
             )
 
         for t in range(PACK):
-            if t == PACK - 1:
-                nc.scalar.activation(*round_result(160, V), ACT.Relu)
             nc.scalar.activation(result[:, t, :], total[:, t, :], ACT.Relu)
             if t > 0:
                 rows = slice(0 if t == 1 else t, t + 1)
                 nc.sync.dma_start(out_rows[:, rows, :], result[:, rows, :])
 
-        for c0, c1 in ((0, P), (P, 160)):
+        nc.scalar.activation(*round_result(192, V), ACT.Relu)
+        for c0, c1 in ((0, P), (P, 192)):
             nc.vector.tensor_scalar_max(*round_result(c0, c1), 0.0)
         out_codes = tile([P, V], U32, "out_codes")
         out_scales = tile([P, V], U8, "out_scales")

@@ -279,12 +279,12 @@ def tile_picked_zrgcn_relu_po_kernel(
             pair = slice(2 * u, 2 * u + 2)
             copy(grouped[:, pair, m0:m1, :].rearrange("p t m j -> p m j t"), by_tile[:, m0:m1, :, pair])
 
-        round_last(nc.vector.tensor_copy, 0, 0, 80)
-        round_last(nc.scalar.copy, 0, 80, P)
-        round_last(nc.scalar.copy, 1, 88, P)
-        round_last(nc.vector.tensor_copy, 1, 0, 40)
+        round_last(nc.vector.tensor_copy, 0, 0, 96)
+        round_last(nc.scalar.copy, 0, 96, P)
+        round_last(nc.scalar.copy, 1, 72, P)
+        round_last(nc.vector.tensor_copy, 1, 0, 32)
         self_pass(1, grouped, slice(0, 1))
-        round_last(nc.vector.tensor_copy, 1, 40, 88)
+        round_last(nc.vector.tensor_copy, 1, 32, 72)
         for tiles in (slice(1, 2), slice(2, 4)):
             self_pass(1, grouped, tiles)
 

@@ -36,7 +36,7 @@ def tile_picked_zrgcn_relu_po_kernel(
         psum = ctx.enter_context(tc.psum_pool(name="psum", bufs=1))
 
         def tile(shape, dtype, name, tag=None):
-            return keep.tile(shape, dtype, name=name, tag=tag or name, align_bytes=64)
+            return keep.tile(shape, dtype, name=name, tag=tag or name, align_bytes=256)
 
         offsets = keep.tile([P, LIST_COLS], U16, name="offsets")
         table_scales = tile([P, T], U8, "table_scales")

@@ -35,13 +35,13 @@ def tile_picked_zrgcn_relu_po_kernel(
         keep = ctx.enter_context(tc.tile_pool(name="keep", bufs=1))
         psum = ctx.enter_context(tc.psum_pool(name="psum", bufs=1))
 
-        def tile(shape, dtype, name, tag=None):
-            return keep.tile(shape, dtype, name=name, tag=tag or name, align_bytes=256)
+        def tile(shape, dtype, name, align=256):
+            return keep.tile(shape, dtype, name=name, tag=name, align_bytes=align)
 
         offsets = keep.tile([P, LIST_COLS], U16, name="offsets")
-        table_scales = tile([P, T], U8, "table_scales")
+        table_scales = tile([P, T], U8, "table_scales", 1024)
         nc.vector.memset(table_scales[:].bitcast(I32), 0)
-        gate_rows = tile([P, V], F32, "gate_rows")
+        gate_rows = tile([P, V], F32, "gate_rows", 1024)
         nc.gpsimd.memset(gate_rows[:], 0.0)
         identity = tile([P, P], F32, "identity")
         make_identity(nc, identity[:])
@@ -51,13 +51,13 @@ def tile_picked_zrgcn_relu_po_kernel(
             nc.sync.dma_start(words[:, c0:c1].bitcast(I32), rows[:, c0:c1])
 
         def load_weight(d, o):
-            raw = tile([P, PACK, N], F32, "raw%d_%d" % (d, o))
+            raw = tile([P, PACK, N], F32, "raw%d_%d" % (d, o), 4096)
             rows = weights[d][o * K_PASS : (o + 1) * K_PASS, :]
             nc.sync.dma_start(raw[:], rows.rearrange("(p j) c -> p j c", j=PACK))
             return raw
 
         raws = {}
-        tables = [tile([P, T], U32, "table%d" % o) for o in range(PASSES)]
+        tables = [tile([P, T], U32, "table%d" % o, 4096) for o in range(PASSES)]
         load_table(tables[0], 0, 0, T // 2)
         nc.sync.dma_start(offsets[:], offs)
         nc.scalar.dma_start(gate_rows[0:D, :], gate[:, 0, :])
@@ -75,9 +75,9 @@ def tile_picked_zrgcn_relu_po_kernel(
             nc.scalar.activation(edges[d][:], gate_bank[:, :, d : d + 1], ACT.Copy)
 
         picked_words = [tile([P, S], U32, "picked_words%d" % o) for o in range(PASSES)]
-        spread_scales = tile([P, S], U8, "spread_scales")
+        spread_scales = tile([P, S], U8, "spread_scales", 1024)
         nc.vector.tensor_copy(spread_scales[:], table_scales[:].indirect(offsets[:]))
-        picked_scales = tile([P, S], U8, "picked_scales")
+        picked_scales = tile([P, S], U8, "picked_scales", 1024)
         nc.vector.tensor_copy(picked_scales[:].bitcast(I32), spread_scales[:].bitcast(I32))
         for o in range(PASSES):
             for r in range(1, 4):
@@ -308,7 +308,7 @@ def tile_picked_zrgcn_relu_po_kernel(
             nc.vector.tensor_tensor(total[:, t, cols], self_banks[t][:, cols], neighbours[t][:, h, :], ALU.add)
 
         out_rows = out_0.rearrange("(p t) v -> p t v", t=PACK)
-        result = tile([P, PACK, V], F32, "result")
+        result = tile([P, PACK, V], F32, "result", 1024)
         rounded = tile([P, V, PACK], BF16, "rounded")
 
         def round_result(c0, c1):
@@ -326,7 +326,7 @@ def tile_picked_zrgcn_relu_po_kernel(
         nc.scalar.activation(*round_result(192, V), ACT.Relu)
         for c0, c1 in ((0, P), (P, 192)):
             nc.vector.tensor_scalar_max(*round_result(c0, c1), 0.0)
-        out_codes = tile([P, V], U32, "out_codes")
+        out_codes = tile([P, V], U32, "out_codes", 1024)
         out_scales = tile([P, V], U8, "out_scales")
         words_out = out_1[0].rearrange("p c r -> p (c r)").bitcast(I32)
         for h in range(HALVES):

from contextlib import ExitStack

import concourse.mybir as mybir
from concourse.masks import make_identity

K, T, S, V, D, N = 1024, 4096, 1024, 256, 3, 512
FLOPS = 2 * K * N * S

F32 = mybir.dt.float32
BF16 = mybir.dt.bfloat16
I32 = mybir.dt.int32
U32 = mybir.dt.uint32
U16 = mybir.dt.uint16
U8 = mybir.dt.uint8
FP8X4 = mybir.dt.float8_e4m3fn_x4
ALU = mybir.AluOpType
ACT = mybir.ActivationFunctionType

P = 128
PACK = 4
K_PASS = P * PACK
PASSES = K // K_PASS
HALVES = V // P
QUADS = 4
LIST_COLS = S // 16


def tile_picked_zrgcn_relu_po_kernel(
    tc, x_words, x_scales, w0, w1, w2, w3, gate, offs, out_0, out_1, out_2
):
    nc = tc.nc
    weights = [w0, w1, w2, w3]

    with ExitStack() as ctx:
        keep = ctx.enter_context(tc.tile_pool(name="keep", bufs=1))
        psum = ctx.enter_context(tc.psum_pool(name="psum", bufs=1))

        def tile(shape, dtype, name, align=256):
            return keep.tile(shape, dtype, name=name, tag=name, align_bytes=align)

        offsets = keep.tile([P, LIST_COLS], U16, name="offsets")
        table_scales = tile([P, T], U8, "table_scales", 1024)
        nc.vector.memset(table_scales[:].bitcast(I32), 0)
        gate_rows = tile([P, V], F32, "gate_rows", 1024)
        nc.gpsimd.memset(gate_rows[:], 0.0)
        identity = tile([P, P], F32, "identity")
        make_identity(nc, identity[:])

        def load_table(words, o, c0, c1):
            rows = x_words[o].rearrange("p c r -> p (c r)").bitcast(I32)
            nc.sync.dma_start(words[:, c0:c1].bitcast(I32), rows[:, c0:c1])

        def load_weight(d, o):
            raw = tile([P, PACK, N], F32, "raw%d_%d" % (d, o), 4096)
            rows = weights[d][o * K_PASS : (o + 1) * K_PASS, :]
            nc.sync.dma_start(raw[:], rows.rearrange("(p j) c -> p j c", j=PACK))
            return raw

        raws = {}
        tables = [tile([P, T], U32, "table%d" % o, 4096) for o in range(PASSES)]
        load_table(tables[0], 0, 0, T // 2)
        nc.sync.dma_start(offsets[:], offs)
        nc.scalar.dma_start(gate_rows[0:D, :], gate[:, 0, :])
        for o in range(PASSES):
            nc.sync.dma_start(table_scales[4 * o : P : 8, :].bitcast(I32), x_scales[o].bitcast(I32))
        load_table(tables[0], 0, T // 2, T)
        raws[1, 0] = load_weight(1, 0)
        load_table(tables[1], 1, 0, T)

        gate_bank = psum.tile([P, HALVES, P], F32, name="gate_bank", tag="bank6")
        for h in range(HALVES):
            nc.tensor.transpose(gate_bank[:, h, :], gate_rows[:, h * P : (h + 1) * P], identity[:])
        edges = [tile([P, HALVES, 1], F32, "edges%d" % d) for d in range(D)]
        for d in range(D):
            nc.scalar.activation(edges[d][:], gate_bank[:, :, d : d + 1], ACT.Copy)

        picked_words = [tile([P, S], U32, "picked_words%d" % o) for o in range(PASSES)]
        spread_scales = tile([P, S], U8, "spread_scales", 1024)
        nc.vector.tensor_copy(spread_scales[:], table_scales[:].indirect(offsets[:]))
        picked_scales = tile([P, S], U8, "picked_scales", 1024)
        nc.vector.tensor_copy(picked_scales[:].bitcast(I32), spread_scales[:].bitcast(I32))
        for o in range(PASSES):
            for r in range(1, 4):
                nc.scalar.dma_start(
                    picked_scales[4 * o + r : P : 32, :].bitcast(I32),
                    spread_scales[4 * o + 8 * r : P : 32, :].bitcast(I32),
                )
        nc.vector.tensor_copy(picked_words[0][:], tables[0][:].indirect(offsets[:]))
        for d, o in [(1, 1), (2, 0), (2, 1), (3, 0), (3, 1), (0, 0), (0, 1)]:
            raws[d, o] = load_weight(d, o)

        def round_relation(d, o, split):
            raw = raws[d, o]
            grouped = tile([P, N, PACK], BF16, "grouped%d_%d" % (d, o))
            for copy, c0, c1 in ((nc.vector.tensor_copy, 0, split), (nc.scalar.copy, split, N)):
                copy(
                    grouped[:, c0:c1, :].rearrange("p (c i) j -> p c j i", i=4),
                    raw[:, :, c0:c1].rearrange("p j (c i) -> p c j i", i=4),
                )
            return grouped

        def relation_pass(d, o, banks, grouped):
            codes = tile([P, N], U32, "codes%d_%d" % (d, o))
            scales = tile([P, N], U8, "scales%d_%d" % (d, o))
            nc.vector.quantize_mx(
                out=codes[:].bitcast(FP8X4), scales=scales[:], in_=grouped[:].rearrange("p c j -> p (c j)")
            )
            for h in range(HALVES):
                cols = slice(d * V + h * P, d * V + (h + 1) * P)
                nc.tensor.matmul_mx(
                    out=banks[h][:],
                    lhsT=picked_words[o][:, cols].bitcast(FP8X4),
                    lhsT_scale=picked_scales[4 * o :, cols],
                    rhs=codes[:].bitcast(FP8X4),
                    rhs_scale=scales[:],
                    start=(o == 0),
                    stop=(o == PASSES - 1),
                )
            return codes, scales

        def relation_banks(label, first):
            return [psum.tile([P, N], F32, name="%s%d" % (label, h), tag="bank%d" % (first + h)) for h in range(HALVES)]

        def dealt(bank):
            return bank[:].rearrange("v (m t) -> v t m", t=PACK)

        def spent_columns(raw):
            return [raw[:, :, N - (h + 1) * P : N - h * P] for h in range(HALVES)]

        def gate_on_scalar(d, banks, terms, h):
            nc.scalar.activation(terms[h], dealt(banks[h]), ACT.Copy, scale=edges[d - 1][:, h, :])

        turned = [psum.tile([P, 2, V], F32, name="turned%d" % u, tag="bank%d" % (4 + u)) for u in range(2)]

        def turn(term, h, first=False, last=False, tiles=range(PACK)):
            for t in tiles:
                nc.tensor.matmul(
                    turned[t // 2][:, t % 2, h * P : (h + 1) * P],
                    term[:, t, :],
                    identity[:],
                    is_transpose=True,
                    start=(first and t % 2 == 0),
                    stop=(last and t % 2 == 1),
                )

        banks1 = relation_banks("one", 0)
        banks2 = relation_banks("two", 2)
        relation_pass(1, 0, banks1, round_relation(1, 0, 256))
        for u in range(2):
            entries = slice(u * (S // 2), (u + 1) * (S // 2))
            list_cols = slice(u * (LIST_COLS // 2), (u + 1) * (LIST_COLS // 2))
            nc.vector.tensor_copy(picked_words[1][:, entries], tables[1][:].indirect(offsets[:, list_cols]))
        codes11 = relation_pass(1, 1, banks1, round_relation(1, 1, 320))

        grouped = round_relation(2, 0, 384)
        terms1 = spent_columns(raws[2, 0])
        for h in range(HALVES):
            gate_on_scalar(1, banks1, terms1, h)
        codes20 = relation_pass(2, 0, banks2, grouped)
        turn(terms1[1], 1, first=True)
        codes21 = relation_pass(2, 1, banks2, round_relation(2, 1, 320))

        def round_dealt(copy, grouped, raw, u, m0, m1):
            pair = slice(2 * u, 2 * u + 2)
            by_tile = raw[:].rearrange("p j (m t) -> p m j t", t=PACK)
            copy(grouped[:, pair, m0:m1, :].rearrange("p t m j -> p m j t"), by_tile[:, m0:m1, :, pair])

        def warm_up(name, words, plane, width, bank):
            unread = psum.tile([P, width], F32, name=name, tag=bank)
            nc.tensor.matmul_mx(
                out=unread[:],
                lhsT=words[:, 0:P].bitcast(FP8X4),
                lhsT_scale=plane[:, 0:P],
                rhs=words[:, 0:width].bitcast(FP8X4),
                rhs_scale=plane[:, 0:width],
                start=True,
                stop=True,
            )

        second_pair = psum.tile([P, HALVES, V], F32, name="three1", tag="bank1")
        banks3 = [
            [psum.tile([P, V], F32, name="three0_%d" % h, tag="bank%d" % (0, 6)[h])[:] for h in range(HALVES)],
            [second_pair[:, h, :] for h in range(HALVES)],
        ]

        def last_relation(o, u, grouped, codes, scales):
            pair = slice(2 * u, 2 * u + 2)
            words = codes[:, pair].rearrange("p t m -> p (t m)").bitcast(FP8X4)
            plane = scales[:, pair].rearrange("p t m -> p (t m)")
            nc.vector.quantize_mx(out=words, scales=plane, in_=grouped[:, pair].rearrange("p t m j -> p (t m j)"))
            for h in range(HALVES):
                cols = slice(3 * V + h * P, 3 * V + (h + 1) * P)
                nc.tensor.matmul_mx(
                    out=banks3[u][h],
                    lhsT=picked_words[o][:, cols].bitcast(FP8X4),
                    lhsT_scale=picked_scales[4 * o :, cols],
                    rhs=words,
                    rhs_scale=plane,
                    start=(o == 0 and (u == 0 or h == 0)),
                    stop=(o == PASSES - 1 and (u == 0 or h == 1)),
                )

        raw = raws[3, 0]
        grouped = tile([P, PACK, P, PACK], BF16, "grouped3_0")
        by_tile = raw[:].rearrange("p j (m t) -> p m j t", t=PACK)
        for copy, m0, m1 in ((nc.vector.tensor_copy, 0, 32), (nc.vector.tensor_copy, 32, 72)):
            copy(grouped[:, :, m0:m1, :].rearrange("p t m j -> p m j t"), by_tile[:, m0:m1])
        for u in range(2):
            round_dealt(nc.scalar.copy, grouped, raw, u, 72, P)
        sum2 = raw[:, :, 0:P]
        nc.vector.scalar_tensor_tensor(sum2, dealt(banks2[0]), edges[1][:, 0, :], terms1[0], ALU.mult, ALU.add)
        warm_up("unread2", codes21[0][:], codes21[1][:], N, "bank2")
        turn(sum2, 0)
        spent = raw[:, :, N - P : N]
        gate_on_scalar(2, banks2, [None, spent], 1)
        turn(spent, 1)
        codes30 = tile([P, PACK, P], U32, "codes3_0")
        scales30 = tile([P, PACK, P], U8, "scales3_0")
        for u in range(2):
            last_relation(0, u, grouped, codes30, scales30)
        raw = raws[3, 1]
        grouped = tile([P, PACK, P, PACK], BF16, "grouped3_1")
        for u in range(2):
            round_dealt(nc.vector.tensor_copy, grouped, raw, u, 0, 80)
            round_dealt(nc.scalar.copy, grouped, raw, u, 80, P)
        codes = tile([P, PACK, P], U32, "codes3_1")
        scales = tile([P, PACK, P], U8, "scales3_1")
        for u in range(2):
            last_relation(1, u, grouped, codes, scales)

        terms3 = [tile([P, PACK, P], F32, "terms3_%d" % h)[:] for h in range(HALVES)]
        for u in range(2):
            pair = slice(2 * u, 2 * u + 2)
            for h in range(HALVES):
                sums = banks3[u][h].rearrange("v (t m) -> v t m", t=2)
                nc.scalar.activation(terms3[h][:, pair], sums, ACT.Copy, scale=edges[2][:, h, :])
                turn(terms3[h], h, last=(h == 1), tiles=range(2 * u, 2 * u + 2))

        warm_up("unread0", codes[:].rearrange("p t m -> p (t m)"), scales[:].rearrange("p t m -> p (t m)"), V, "bank1")

        self_codes = [tile([P, PACK, P], U32, "self_codes%d" % o) for o in range(PASSES)]
        self_scales = [tile([P, PACK, P], U8, "self_scales%d" % o) for o in range(PASSES)]
        self_banks = [psum.tile([P, V], F32, name="self_bank%d" % t, tag="bank%d" % (6, 7, 2, 3)[t]) for t in range(PACK)]

        first_halves = [self_banks[0][:, :P], psum.tile([P, P], F32, name="self_bank0_1", tag="bank0")[:]]

        def self_pass(o, grouped, tiles):
            nc.vector.quantize_mx(
                out=self_codes[o][:, tiles, :].rearrange("p t m -> p (t m)").bitcast(FP8X4),
                scales=self_scales[o][:, tiles, :].rearrange("p t m -> p (t m)"),
                in_=grouped[:, tiles].rearrange("p t m j -> p (t m j)"),
            )
            for t in range(tiles.start, tiles.stop):
                pieces = [(self_banks[t][:], 0, V)]
                if t == 0:
                    pieces = [(first_halves[h], h * P, (h + 1) * P) for h in range(HALVES)]
                for bank, v0, v1 in pieces:
                    nc.tensor.matmul_mx(
                        out=bank,
                        lhsT=self_codes[o][:, t, :].bitcast(FP8X4),
                        lhsT_scale=self_scales[o][:, t, :],
                        rhs=picked_words[o][:, v0:v1].bitcast(FP8X4),
                        rhs_scale=picked_scales[4 * o :, v0:v1],
                        start=(o == 0),
                        stop=(o == PASSES - 1),
                    )

        grouped = tile([P, PACK, P, PACK], BF16, "self_grouped0")
        by_tile = raws[0, 0][:].rearrange("p j (m t) -> p m j t", t=PACK)
        for tiles, m0, m1 in ((slice(0, 4), 0, 96), (slice(0, 2), 96, P), (slice(2, 4), 96, P)):
            nc.vector.tensor_copy(grouped[:, tiles, m0:m1, :].rearrange("p t m j -> p m j t"), by_tile[:, m0:m1, :, tiles])
        for u in range(2):
            self_pass(0, grouped, slice(2 * u, 2 * u + 2))

        grouped = tile([P, PACK, P, PACK], BF16, "self_grouped1")
        by_tile = raws[0, 1][:].rearrange("p j (m t) -> p m j t", t=PACK)

        def round_last(copy, u, m0, m1):
            pair = slice(2 * u, 2 * u + 2)
            copy(grouped[:, pair, m0:m1, :].rearrange("p t m j -> p m j t"), by_tile[:, m0:m1, :, pair])

        round_last(nc.vector.tensor_copy, 0, 0, 96)
        round_last(nc.scalar.copy, 0, 96, P)
        round_last(nc.scalar.copy, 1, 72, P)
        round_last(nc.vector.tensor_copy, 1, 0, 32)
        self_pass(1, grouped, slice(0, 1))
        round_last(nc.vector.tensor_copy, 1, 32, 72)
        for tiles in (slice(1, 2), slice(2, 4)):
            self_pass(1, grouped, tiles)

        def by_halves(ap):
            return ap.rearrange("p (h v) -> p h v", h=HALVES)

        summed = tile([P, PACK, V], F32, "summed")
        for u in range(2):
            nc.scalar.copy(summed[:, 2 * u : 2 * u + 2, :], turned[u][:])
        neighbours = [by_halves(summed[:, t, :]) for t in range(PACK)]

        total = tile([P, PACK, V], F32, "total")
        for h in range(HALVES):
            cols = slice(h * P, (h + 1) * P)
            nc.vector.tensor_tensor(total[:, 0, cols], first_halves[h], neighbours[0][:, h, :], ALU.add)
        for t in range(1, PACK - 1):
            nc.vector.tensor_tensor(by_halves(total[:, t, :]), by_halves(self_banks[t][:]), neighbours[t], ALU.add)
        t = PACK - 1
        for h in range(HALVES):
            cols = slice(h * P, (h + 1) * P)
            nc.vector.tensor_tensor(total[:, t, cols], self_banks[t][:, cols], neighbours[t][:, h, :], ALU.add)

        out_rows = out_0.rearrange("(p t) v -> p t v", t=PACK)
        result = tile([P, PACK, V], F32, "result", 1024)
        rounded = tile([P, V, PACK], BF16, "rounded")

        def round_result(c0, c1):
            return (
                rounded[:, c0:c1, :].rearrange("p (c i) t -> p c t i", i=4),
                total[:, :, c0:c1].rearrange("p t (c i) -> p c t i", i=4),
            )

        for t in range(PACK):
            nc.scalar.activation(result[:, t, :], total[:, t, :], ACT.Relu)
            if t > 0:
                rows = slice(0 if t == 1 else t, t + 1)
                nc.sync.dma_start(out_rows[:, rows, :], result[:, rows, :])

        nc.scalar.activation(*round_result(192, V), ACT.Relu)
        for c0, c1 in ((0, P), (P, 192)):
            nc.vector.tensor_scalar_max(*round_result(c0, c1), 0.0)
        out_codes = tile([P, V], U32, "out_codes", 1024)
        out_scales = tile([P, V], U8, "out_scales")
        words_out = out_1[0].rearrange("p c r -> p (c r)").bitcast(I32)
        for h in range(HALVES):
            cols = slice(h * P, (h + 1) * P)
            nc.vector.quantize_mx(
                out=out_codes[:, cols].bitcast(FP8X4),
                scales=out_scales[:, cols],
                in_=rounded[:, cols, :].rearrange("p c t -> p (c t)"),
            )
        nc.sync.dma_start(words_out, out_codes[:].bitcast(I32))
        for q in range(QUADS):
            queue = nc.sync if q < 2 else nc.scalar
            queue.dma_start(out_2[0, 4 * q : 4 * q + 4, :].bitcast(I32), out_scales[32 * q : 32 * q + 4, :].bitcast(I32))
